import numpy as np
import ml_dtypes


def mxq(x, axis, fmt="e4m3"):
    dtype, down = {"e4m3": (ml_dtypes.float8_e4m3fn, 7), "e5m2": (ml_dtypes.float8_e5m2, 14)}[fmt]
    v = np.moveaxis(np.asarray(x, np.float32).astype(ml_dtypes.bfloat16).astype(np.float64), axis, -1)
    blocks = v.reshape(v.shape[:-1] + (-1, 32))
    amax = np.abs(blocks).max(-1, keepdims=True)
    byte = np.maximum(np.where(amax > 0, np.frexp(amax)[1] - 1 + 127, 0) - down, 1)
    scale = np.exp2(byte - 127.0)
    codes = (blocks / scale).astype(np.float32).astype(dtype).astype(np.float64)
    return np.moveaxis((codes * scale).reshape(v.shape), -1, axis)


WIDE = False


def mx_kscale(k):
    if not WIDE:
        return np.ones(k)
    levels = np.array([10, -10, 5, -5, 0])
    if k % 512:
        return np.exp2(np.random.permutation(np.resize(levels, k // 32))).repeat(32)
    a = np.empty((k // 512, 16))
    for p in range(k // 512):
        a[p, :8] = np.random.permutation(np.resize(levels, 8))
        for g in range(8):
            far = levels[np.abs(levels - a[p, g]) >= 10]
            a[p, g + 8] = far[np.random.randint(len(far))]
    return np.exp2(a.ravel()).repeat(32)


def f64(x):
    return np.asarray(x).astype(np.float64)


def striped(idx):
    return np.tile(idx.reshape(-1, 16).T, (8, 1)).astype(np.uint16)


def unstriped(offs):
    return offs[:16].T.reshape(-1).astype(np.int64)


def relu2(v):
    return np.maximum(v, 0.0) ** 2


K, T, E, C, N = 2560, 512, 4, 256, 384


def by_expert(wq, xq):
    return np.concatenate([wq[e].T @ xq[:, e * C:(e + 1) * C] for e in range(E)], axis=1)


def setup_inputs():
    n = np.random.standard_normal
    s = mx_kscale(K)[:, None]
    first = np.random.permutation(np.repeat(np.arange(E), T // E))
    second = (first + 1 + np.random.permutation(np.repeat(np.arange(E - 1), -(-T // (E - 1)))[:T])) % E
    while np.bincount(second, minlength=E).max() != T // E:
        load = np.bincount(second, minlength=E); hi, lo = int(load.argmax()), int(load.argmin())
        t = np.flatnonzero((second == hi) & (first != lo))[0]; second[t] = lo
    slot_token = np.empty(E * C, np.int64); pos = np.empty((2, T), np.int64); fill = np.zeros(E, np.int64)
    place = np.stack([np.random.permutation(C) for _ in range(E)])
    for r, deal in enumerate((first, second)):
        for t in np.random.permutation(T):
            e = deal[t]; j = e * C + place[e, fill[e]]; fill[e] += 1; slot_token[j] = t; pos[r, t] = j
    g = np.random.uniform(0.2, 0.8, T)
    return {
        "xT": (n((K, T)) * s).astype(np.float32),
        "w": (n((E, K, N)) / np.sqrt(K) / s[None]).astype(np.float32),
        "b": (0.3 * n((N, E))).astype(np.float32),
        "gate": np.stack([np.tile(g, (N, 1)), np.tile(1.0 - g, (N, 1))]).astype(np.float32),
        "offs": striped(slot_token),
        "pos1": striped(pos[0]),
        "pos2": striped(pos[1]),
    }


def reference(xT, w, b, gate, offs, pos1, pos2):
    idx = unstriped(offs)
    xq = mxq(f64(xT)[:, idx], 0, "e4m3")
    y = by_expert(mxq(f64(w), 1, "e4m3"), xq)
    y = relu2(y + np.repeat(f64(b), C, axis=1))
    return f64(gate[0]) * y[:, unstriped(pos1)] + f64(gate[1]) * y[:, unstriped(pos2)]

@@ -1,0 +1,228 @@
+from contextlib import ExitStack
+
+import concourse.mybir as mybir
+from concourse.masks import make_identity
+
+K, T, E, C, N = 2560, 512, 4, 256, 384
+
+F32 = mybir.dt.float32
+BF16 = mybir.dt.bfloat16
+U32 = mybir.dt.uint32
+U16 = mybir.dt.uint16
+U8 = mybir.dt.uint8
+FP8X4 = mybir.dt.float8_e4m3fn_x4
+RELU = mybir.ActivationFunctionType.Relu
+SQUARE = mybir.ActivationFunctionType.Square
+MULT = mybir.AluOpType.mult
+ADD = mybir.AluOpType.add
+
+P = 128
+PACK = 4
+PASSES = K // (P * PACK)
+BLOCKS = N // P
+SLOTS = E * C
+LIST_ROWS = 16
+
+FLOPS = 2 * K * N * E * C
+
+SLOT_SLICES = ((0, 384), (384, 768), (768, 1024))
+
+PLANES_PER_TILE = 4
+
+FIRST_PASS_CUTS = ((0, T // 2), (T // 2, T))
+
+X_SCALAR_SHARE = (1, 1, 2 / 3, 1, 1 / 2)
+W_SCALAR_SHARE = (1,) * 10 + (1 / 2,) + (0,) * 4 + (1 / 2, 0, 0, 1 / 3)
+LAST_SCALAR_SHARE = (1, 2 / 3, 1 / 3)
+
+GROUPS = ((0, 1), (2, 3), (4, 5), (6, 7), (8, 9), (10, 11), (12, 13), (14,), (15, 16), (17, 18), (19,))
+
+GATHERS_PER_UNIT = 4
+
+RAW_BUFS = 12
+GROUPED_BUFS = 6
+CODE_BUFS = 6
+
+
+def interleave(nc, grouped, raw, scalar_share):
+    dst = grouped.rearrange("p (c i t) -> p c t i", i=4, t=PACK)
+    src = raw.rearrange("p t (c i) -> p c t i", i=4)
+    quads = dst.shape[1]
+    cut = int(quads * scalar_share + 0.5)
+    if cut > 0:
+        nc.scalar.copy(out=dst[:, :cut], in_=src[:, :cut])
+    if cut < quads:
+        nc.vector.tensor_copy(out=dst[:, cut:], in_=src[:, cut:])
+
+
+def power_of_two_pieces(width):
+    pieces, lo = [], 0
+    for piece in (512, 256, 128):
+        while width - lo >= piece:
+            pieces.append((lo, lo + piece))
+            lo += piece
+    return pieces
+
+
+def tile_routed_moe_kernel(tc, xT, w, b, gate, offs, pos1, pos2, out):
+    nc = tc.nc
+    with ExitStack() as ctx:
+        keep = ctx.enter_context(tc.tile_pool(name="keep", bufs=1))
+        ring = ctx.enter_context(tc.tile_pool(name="ring", bufs=2))
+        psum = ctx.enter_context(tc.psum_pool(name="psum", bufs=8))
+
+        x_rows = xT.rearrange("(a p j) t -> a p j t", p=P, j=PACK)
+        w_rows = w.rearrange("e (a p j) n -> e a p j n", p=P, j=PACK)
+
+        offs_list = keep.tile([P, SLOTS // LIST_ROWS], U16, name="offs_list")
+        pos1_list = keep.tile([P, T // LIST_ROWS], U16, name="pos1_list")
+        pos2_list = keep.tile([P, T // LIST_ROWS], U16, name="pos2_list")
+        bias = keep.tile([P, BLOCKS, E], F32, name="bias")
+
+        identity = keep.tile([P, P], F32, name="identity")
+        make_identity(nc, identity[:])
+
+        token_scales, slot_scales = [], []
+        for i in range(0, PASSES, PLANES_PER_TILE):
+            tokens = keep.tile([P, T], U8, name=f"token_scales{i}", align_bytes=64)
+            slots = keep.tile([P, SLOTS], U8, name=f"slot_scales{i}", align_bytes=64)
+            nc.gpsimd.memset(tokens[:], 0)
+            token_scales.append(tokens)
+            slot_scales.append(slots)
+
+        x_raw = []
+        for a in range(PASSES):
+            raw = ring.tile([P, PACK, T], F32, name="x_raw", tag="raw", bufs=RAW_BUFS)
+            for lo, hi in FIRST_PASS_CUTS if a == 0 else ((0, T),):
+                nc.sync.dma_start(out=raw[:, :, lo:hi], in_=x_rows[a, :, :, lo:hi])
+            x_raw.append(raw)
+            if a == 0:
+                nc.sync.dma_start(out=offs_list[:], in_=offs)
+            if a == 2:
+                nc.sync.dma_start(out=bias[:], in_=b.rearrange("(n p) e -> p n e", p=P))
+
+        token_codes = []
+        for a in range(PASSES):
+            grouped = ring.tile([P, T * PACK], BF16, name="x_grouped", tag="grouped", bufs=GROUPED_BUFS, align_bytes=64)
+            for lo, hi in FIRST_PASS_CUTS if a == 0 else ((0, T),):
+                interleave(nc, grouped[:, PACK * lo : PACK * hi], x_raw[a][:, :, lo:hi], X_SCALAR_SHARE[a])
+            codes = keep.tile([P, T], U32, name=f"token_codes{a}", align_bytes=64)
+            plane = PACK * (a % PLANES_PER_TILE)
+            nc.vector.quantize_mx(
+                out=codes[:].bitcast(FP8X4), scales=token_scales[a // PLANES_PER_TILE][plane:P, :], in_=grouped[:]
+            )
+            token_codes.append(codes)
+
+        slot_codes, gathers = [], []
+        for a in range(PASSES):
+            codes = keep.tile([P, SLOTS], U32, name=f"slot_codes{a}", align_bytes=64)
+            slot_codes.append(codes)
+            moves = [(codes, token_codes[a])]
+            if a % PLANES_PER_TILE == PLANES_PER_TILE - 1 or a == PASSES - 1:
+                moves.append((slot_scales[a // PLANES_PER_TILE], token_scales[a // PLANES_PER_TILE]))
+            for dst, window in moves:
+                for lo, hi in SLOT_SLICES:
+                    gathers.append((dst, window, lo, hi))
+
+        def gather_some():
+            for dst, window, lo, hi in gathers[:GATHERS_PER_UNIT]:
+                offsets = offs_list[:, lo // LIST_ROWS : hi // LIST_ROWS]
+                nc.vector.tensor_copy(out=dst[:, lo:hi], in_=window[:].indirect(offsets))
+            return gathers[GATHERS_PER_UNIT:]
+
+        def multiply(sums, e, a, codes, scales):
+            slots = slice(e * C, (e + 1) * C)
+            plane = PACK * (a % PLANES_PER_TILE)
+            nc.tensor.matmul_mx(
+                out=sums,
+                lhsT=codes.bitcast(FP8X4),
+                lhsT_scale=scales,
+                rhs=slot_codes[a][:, slots].bitcast(FP8X4),
+                rhs_scale=slot_scales[a // PLANES_PER_TILE][plane:P, slots],
+                start=(a == 0),
+                stop=(a == PASSES - 1),
+            )
+
+        y = []
+        for n in range(BLOCKS):
+            y_block = keep.tile([P, SLOTS], F32, name=f"y{n}")
+            y.append(y_block)
+
+        def relu(sums, e, n):
+            nc.scalar.activation(
+                out=y[n][:, e * C : (e + 1) * C], in_=sums, func=RELU, bias=bias[:, n, e : e + 1]
+            )
+
+        def square(n, first_expert, last_expert):
+            part = y[n][:, first_expert * C : (last_expert + 1) * C]
+            nc.scalar.activation(out=part, in_=part, func=SQUARE)
+
+        sums = {}
+        for n in range(BLOCKS):
+            pair = psum.tile([P, 2 * C], F32, name="pair", tag="bank")
+            sums[(0, n)] = pair[:, 0:C]
+            sums[(1, n)] = pair[:, C : 2 * C]
+
+        waiting = []
+        for group in GROUPS:
+            width = len(group) * N
+            last = group == GROUPS[-1]
+            grouped = ring.tile([P, width * PACK], BF16, name="w_grouped", tag="grouped", bufs=GROUPED_BUFS, align_bytes=64)
+            codes = ring.tile([P, width], U32, name="w_codes", tag="w_codes", bufs=CODE_BUFS, align_bytes=64)
+            scales = ring.tile([P, width], U8, name="w_scales", tag="w_scales", bufs=CODE_BUFS, align_bytes=64)
+            for i, unit in enumerate(group):
+                e, a = unit // PASSES, unit % PASSES
+                raw = ring.tile([P, PACK, N], F32, name="w_raw", tag="raw", bufs=RAW_BUFS)
+                nc.sync.dma_start(out=raw[:], in_=w_rows[e, a])
+                shares = LAST_SCALAR_SHARE if last else (W_SCALAR_SHARE[unit],)
+                step = N // len(shares)
+                for part, share in enumerate(shares):
+                    lo = part * step
+                    at = PACK * (i * N + lo)
+                    interleave(nc, grouped[:, at : at + PACK * step], raw[:, :, lo : lo + step], share)
+                gathers = gather_some()
+                waiting.append((e, a, codes[:, i * N : (i + 1) * N], scales[:, i * N : (i + 1) * N]))
+            pieces = [(n * P, (n + 1) * P) for n in range(BLOCKS)] if last else power_of_two_pieces(width)
+            for lo, hi in pieces:
+                nc.vector.quantize_mx(
+                    out=codes[:, lo:hi].bitcast(FP8X4), scales=scales[:, lo:hi], in_=grouped[:, PACK * lo : PACK * hi]
+                )
+            if len(gathers) > 0:
+                continue
+            for e, a, unit_codes, unit_scales in waiting:
+                for n in range(BLOCKS):
+                    if e > 1 and a == 0:
+                        bank = psum.tile([P, C], F32, name="bank", tag="bank")
+                        sums[(e, n)] = bank[:]
+                    features = slice(n * P, (n + 1) * P)
+                    multiply(sums[(e, n)], e, a, unit_codes[:, features], unit_scales[:, features])
+                if e > 0 and a == PASSES - 1:
+                    for n in range(BLOCKS):
+                        if e == 1:
+                            relu(sums[(0, n)], 0, n)
+                        relu(sums[(e, n)], e, n)
+                        square(n, 0 if e == 1 else e, e)
+            waiting.clear()
+
+        nc.sync.dma_start(out=pos1_list[:], in_=pos1)
+        nc.sync.dma_start(out=pos2_list[:], in_=pos2)
+        gates = []
+        for n in range(BLOCKS):
+            gate_block = ring.tile([P, 2, T], F32, name="gate_block", tag="raw", bufs=RAW_BUFS)
+            nc.sync.dma_start(out=gate_block[:], in_=gate[:, n * P : (n + 1) * P, :].rearrange("r p t -> p r t"))
+            gates.append(gate_block)
+
+        for n in range(BLOCKS):
+            first = ring.tile([P, T], F32, name="first", tag="first", bufs=BLOCKS)
+            second = ring.tile([P, T], F32, name="second", tag="second", bufs=BLOCKS)
+            nc.vector.tensor_tensor(out=first[:], in0=y[n][:].indirect(pos1_list[:]), in1=gates[n][:, 0, :], op=MULT)
+            nc.vector.tensor_tensor(out=second[:], in0=y[n][:].indirect(pos2_list[:]), in1=gates[n][:, 1, :], op=MULT)
+            result = ring.tile([P, T], F32, name="result", tag="result", bufs=BLOCKS)
+            if n == 0:
+                total = psum.tile([P, T], F32, name="total", tag="bank")
+                nc.tensor.matmul(total[:], identity[:], first[:], start=True, stop=False)
+                nc.tensor.matmul(total[:], identity[:], second[:], start=False, stop=True)
+                nc.scalar.copy(out=result[:], in_=total[:])
+            else:
+                nc.vector.tensor_tensor(out=result[:], in0=first[:], in1=second[:], op=ADD)
+            nc.sync.dma_start(out=out[n * P : (n + 1) * P, :], in_=result[:])

@@ -1,7 +1,6 @@
 from contextlib import ExitStack
 
 import concourse.mybir as mybir
-from concourse.masks import make_identity
 
 K, T, E, C, N = 2560, 512, 4, 256, 384
 
@@ -13,55 +12,42 @@ U8 = mybir.dt.uint8
 FP8X4 = mybir.dt.float8_e4m3fn_x4
 RELU = mybir.ActivationFunctionType.Relu
 SQUARE = mybir.ActivationFunctionType.Square
+COPY = mybir.ActivationFunctionType.Copy
 MULT = mybir.AluOpType.mult
 ADD = mybir.AluOpType.add
+MAX = mybir.AluOpType.max
 
 P = 128
 PACK = 4
 PASSES = K // (P * PACK)
 BLOCKS = N // P
 SLOTS = E * C
+UNITS = E * PASSES
 LIST_ROWS = 16
 
 FLOPS = 2 * K * N * E * C
 
-SLOT_SLICES = ((0, 384), (384, 768), (768, 1024))
-
 PLANES_PER_TILE = 4
+SLOT_SLICES = {1: ((0, 384), (384, 768), (768, 1024)), 2: ((0, 768), (768, 1024)), 3: ((0, 1024),)}
 
-FIRST_PASS_CUTS = ((0, T // 2), (T // 2, T))
-
-X_SCALAR_SHARE = (1, 1, 2 / 3, 1, 1 / 2)
-W_SCALAR_SHARE = (1,) * 10 + (1 / 2,) + (0,) * 4 + (1 / 2, 0, 0, 1 / 3)
-LAST_SCALAR_SHARE = (1, 2 / 3, 1 / 3)
-
-GROUPS = ((0, 1), (2, 3), (4, 5), (6, 7), (8, 9), (10, 11), (12, 13), (14,), (15, 16), (17, 18), (19,))
-
-GATHERS_PER_UNIT = 4
+SCALAR_ALONE_UNITS = 8
+VECTOR_ALONE_UNITS = (10, 11, 12, 15, 16)
+SHARED = 0.4
 
 RAW_BUFS = 12
-GROUPED_BUFS = 6
-CODE_BUFS = 6
+GROUPED_BUFS = 5
+CODE_BUFS = 12
 
 
 def interleave(nc, grouped, raw, scalar_share):
     dst = grouped.rearrange("p (c i t) -> p c t i", i=4, t=PACK)
     src = raw.rearrange("p t (c i) -> p c t i", i=4)
     quads = dst.shape[1]
-    cut = int(quads * scalar_share + 0.5)
+    cut = 2 * int(quads * scalar_share / 2 + 0.5)
     if cut > 0:
         nc.scalar.copy(out=dst[:, :cut], in_=src[:, :cut])
     if cut < quads:
         nc.vector.tensor_copy(out=dst[:, cut:], in_=src[:, cut:])
-
-
-def power_of_two_pieces(width):
-    pieces, lo = [], 0
-    for piece in (512, 256, 128):
-        while width - lo >= piece:
-            pieces.append((lo, lo + piece))
-            lo += piece
-    return pieces
 
 
 def tile_routed_moe_kernel(tc, xT, w, b, gate, offs, pos1, pos2, out):
@@ -79,56 +65,46 @@ def tile_routed_moe_kernel(tc, xT, w, b, gate, offs, pos1, pos2, out):
         pos2_list = keep.tile([P, T // LIST_ROWS], U16, name="pos2_list")
         bias = keep.tile([P, BLOCKS, E], F32, name="bias")
 
-        identity = keep.tile([P, P], F32, name="identity")
-        make_identity(nc, identity[:])
-
-        token_scales, slot_scales = [], []
+        token_codes = keep.tile([P, PASSES * T], U32, name="token_codes", align_bytes=64)
+        token_scales = keep.tile([P, 2 * T], U8, name="token_scales", align_bytes=64)
+        nc.gpsimd.memset(token_scales[:], 0)
+        slot_scales = []
         for i in range(0, PASSES, PLANES_PER_TILE):
-            tokens = keep.tile([P, T], U8, name=f"token_scales{i}", align_bytes=64)
             slots = keep.tile([P, SLOTS], U8, name=f"slot_scales{i}", align_bytes=64)
-            nc.gpsimd.memset(tokens[:], 0)
-            token_scales.append(tokens)
             slot_scales.append(slots)
 
         x_raw = []
         for a in range(PASSES):
             raw = ring.tile([P, PACK, T], F32, name="x_raw", tag="raw", bufs=RAW_BUFS)
-            for lo, hi in FIRST_PASS_CUTS if a == 0 else ((0, T),):
-                nc.sync.dma_start(out=raw[:, :, lo:hi], in_=x_rows[a, :, :, lo:hi])
+            nc.sync.dma_start(out=raw[:], in_=x_rows[a])
             x_raw.append(raw)
             if a == 0:
                 nc.sync.dma_start(out=offs_list[:], in_=offs)
-            if a == 2:
-                nc.sync.dma_start(out=bias[:], in_=b.rearrange("(n p) e -> p n e", p=P))
+        nc.sync.dma_start(out=bias[:], in_=b.rearrange("(n p) e -> p n e", p=P))
 
-        token_codes = []
+        def gather(dst, tokens, start, width):
+            for lo, hi in SLOT_SLICES[width]:
+                offsets = offs_list[:, lo // LIST_ROWS : hi // LIST_ROWS]
+                nc.vector.tensor_copy(out=dst[:, lo:hi], in_=tokens[:, start : start + width * T].indirect(offsets))
+
+        slot_codes = []
         for a in range(PASSES):
             grouped = ring.tile([P, T * PACK], BF16, name="x_grouped", tag="grouped", bufs=GROUPED_BUFS, align_bytes=64)
-            for lo, hi in FIRST_PASS_CUTS if a == 0 else ((0, T),):
-                interleave(nc, grouped[:, PACK * lo : PACK * hi], x_raw[a][:, :, lo:hi], X_SCALAR_SHARE[a])
-            codes = keep.tile([P, T], U32, name=f"token_codes{a}", align_bytes=64)
+            interleave(nc, grouped[:], x_raw[a][:], SHARED if a == 0 else 1)
+            start = (PASSES - 1 - a) * T
             plane = PACK * (a % PLANES_PER_TILE)
+            group = a // PLANES_PER_TILE
+            scale_start = (1 - group) * T
             nc.vector.quantize_mx(
-                out=codes[:].bitcast(FP8X4), scales=token_scales[a // PLANES_PER_TILE][plane:P, :], in_=grouped[:]
+                out=token_codes[:, start : start + T].bitcast(FP8X4),
+                scales=token_scales[plane:P, scale_start : scale_start + T],
+                in_=grouped[:],
             )
-            token_codes.append(codes)
-
-        slot_codes, gathers = [], []
-        for a in range(PASSES):
-            codes = keep.tile([P, SLOTS], U32, name=f"slot_codes{a}", align_bytes=64)
-            slot_codes.append(codes)
-            moves = [(codes, token_codes[a])]
+            slots = keep.tile([P, SLOTS], U32, name=f"slot_codes{a}", align_bytes=64)
+            gather(slots, token_codes, start, min(a + 1, 3))
+            slot_codes.append(slots)
             if a % PLANES_PER_TILE == PLANES_PER_TILE - 1 or a == PASSES - 1:
-                moves.append((slot_scales[a // PLANES_PER_TILE], token_scales[a // PLANES_PER_TILE]))
-            for dst, window in moves:
-                for lo, hi in SLOT_SLICES:
-                    gathers.append((dst, window, lo, hi))
-
-        def gather_some():
-            for dst, window, lo, hi in gathers[:GATHERS_PER_UNIT]:
-                offsets = offs_list[:, lo // LIST_ROWS : hi // LIST_ROWS]
-                nc.vector.tensor_copy(out=dst[:, lo:hi], in_=window[:].indirect(offsets))
-            return gathers[GATHERS_PER_UNIT:]
+                gather(slot_scales[group], token_scales, scale_start, group + 1)
 
         def multiply(sums, e, a, codes, scales):
             slots = slice(e * C, (e + 1) * C)
@@ -148,61 +124,70 @@ def tile_routed_moe_kernel(tc, xT, w, b, gate, offs, pos1, pos2, out):
             y_block = keep.tile([P, SLOTS], F32, name=f"y{n}")
             y.append(y_block)
 
-        def relu(sums, e, n):
-            nc.scalar.activation(
-                out=y[n][:, e * C : (e + 1) * C], in_=sums, func=RELU, bias=bias[:, n, e : e + 1]
-            )
+        def relu(engine, sums, e, n):
+            part = y[n][:, e * C : (e + 1) * C]
+            if engine == "scalar":
+                nc.scalar.activation(out=part, in_=sums, func=RELU, bias=bias[:, n, e : e + 1])
+            else:
+                nc.vector.tensor_scalar(
+                    out=part, in0=sums, scalar1=bias[:, n, e : e + 1], scalar2=0.0, op0=ADD, op1=MAX
+                )
 
-        def square(n, first_expert, last_expert):
+        def square(engine, first_expert, last_expert, n):
             part = y[n][:, first_expert * C : (last_expert + 1) * C]
-            nc.scalar.activation(out=part, in_=part, func=SQUARE)
+            if engine == "scalar":
+                nc.scalar.activation(out=part, in_=part, func=SQUARE)
+            else:
+                nc.vector.tensor_tensor(out=part, in0=part, in1=part, op=MULT)
 
         sums = {}
         for n in range(BLOCKS):
             pair = psum.tile([P, 2 * C], F32, name="pair", tag="bank")
             sums[(0, n)] = pair[:, 0:C]
             sums[(1, n)] = pair[:, C : 2 * C]
-
-        waiting = []
-        for group in GROUPS:
-            width = len(group) * N
-            last = group == GROUPS[-1]
-            grouped = ring.tile([P, width * PACK], BF16, name="w_grouped", tag="grouped", bufs=GROUPED_BUFS, align_bytes=64)
-            codes = ring.tile([P, width], U32, name="w_codes", tag="w_codes", bufs=CODE_BUFS, align_bytes=64)
-            scales = ring.tile([P, width], U8, name="w_scales", tag="w_scales", bufs=CODE_BUFS, align_bytes=64)
-            for i, unit in enumerate(group):
-                e, a = unit // PASSES, unit % PASSES
-                raw = ring.tile([P, PACK, N], F32, name="w_raw", tag="raw", bufs=RAW_BUFS)
-                nc.sync.dma_start(out=raw[:], in_=w_rows[e, a])
-                shares = LAST_SCALAR_SHARE if last else (W_SCALAR_SHARE[unit],)
-                step = N // len(shares)
-                for part, share in enumerate(shares):
-                    lo = part * step
-                    at = PACK * (i * N + lo)
-                    interleave(nc, grouped[:, at : at + PACK * step], raw[:, :, lo : lo + step], share)
-                gathers = gather_some()
-                waiting.append((e, a, codes[:, i * N : (i + 1) * N], scales[:, i * N : (i + 1) * N]))
-            pieces = [(n * P, (n + 1) * P) for n in range(BLOCKS)] if last else power_of_two_pieces(width)
-            for lo, hi in pieces:
-                nc.vector.quantize_mx(
-                    out=codes[:, lo:hi].bitcast(FP8X4), scales=scales[:, lo:hi], in_=grouped[:, PACK * lo : PACK * hi]
-                )
-            if len(gathers) > 0:
-                continue
-            for e, a, unit_codes, unit_scales in waiting:
+        for unit in range(UNITS):
+            e, a = unit // PASSES, unit % PASSES
+            last = unit == UNITS - 1
+            raw = ring.tile([P, PACK, N], F32, name="w_raw", tag="raw", bufs=RAW_BUFS)
+            nc.sync.dma_start(out=raw[:], in_=w_rows[e, a])
+            grouped = ring.tile([P, N * PACK], BF16, name="w_grouped", tag="grouped", bufs=GROUPED_BUFS, align_bytes=64)
+            codes = ring.tile([P, N], U32, name="w_codes", tag="w_codes", bufs=CODE_BUFS, align_bytes=64)
+            scales = ring.tile([P, N], U8, name="w_scales", tag="w_scales", bufs=CODE_BUFS, align_bytes=64)
+            if not last:
+                share = 1 if unit < SCALAR_ALONE_UNITS else 0 if unit in VECTOR_ALONE_UNITS else SHARED
+                pieces = ((0, 2 * P), (2 * P, N)) if share == 0 else ((0, N),)
+                for lo, hi in pieces:
+                    interleave(nc, grouped[:, PACK * lo : PACK * hi], raw[:, :, lo:hi], share)
+                for lo, hi in pieces:
+                    nc.vector.quantize_mx(
+                        out=codes[:, lo:hi].bitcast(FP8X4), scales=scales[:, lo:hi], in_=grouped[:, PACK * lo : PACK * hi]
+                    )
+            else:
+                for n, share in ((0, 0), (1, 1), (2, 0)):
+                    interleave(nc, grouped[:, PACK * n * P : PACK * (n + 1) * P], raw[:, :, n * P : (n + 1) * P], share)
                 for n in range(BLOCKS):
-                    if e > 1 and a == 0:
-                        bank = psum.tile([P, C], F32, name="bank", tag="bank")
-                        sums[(e, n)] = bank[:]
-                    features = slice(n * P, (n + 1) * P)
-                    multiply(sums[(e, n)], e, a, unit_codes[:, features], unit_scales[:, features])
-                if e > 0 and a == PASSES - 1:
-                    for n in range(BLOCKS):
-                        if e == 1:
-                            relu(sums[(0, n)], 0, n)
-                        relu(sums[(e, n)], e, n)
-                        square(n, 0 if e == 1 else e, e)
-            waiting.clear()
+                    nc.vector.quantize_mx(
+                        out=codes[:, n * P : (n + 1) * P].bitcast(FP8X4),
+                        scales=scales[:, n * P : (n + 1) * P],
+                        in_=grouped[:, PACK * n * P : PACK * (n + 1) * P],
+                    )
+            for n in range(BLOCKS):
+                if a == 0 and e > 1:
+                    bank = psum.tile([P, C], F32, name="bank", tag="bank")
+                    sums[(e, n)] = bank[:]
+                features = slice(n * P, (n + 1) * P)
+                multiply(sums[(e, n)], e, a, codes[:, features], scales[:, features])
+            if a == PASSES - 1 and e in (1, 2):
+                first_expert = 0 if e == 1 else e
+                for n in range(BLOCKS):
+                    for done in range(first_expert, e + 1):
+                        relu("scalar", sums[(done, n)], done, n)
+                for n in range(BLOCKS):
+                    square("scalar", first_expert, e, n)
+            if last:
+                for n in range(BLOCKS):
+                    relu("vector", sums[(e, n)], e, n)
+                    square("scalar", e, e, n)
 
         nc.sync.dma_start(out=pos1_list[:], in_=pos1)
         nc.sync.dma_start(out=pos2_list[:], in_=pos2)
@@ -212,17 +197,22 @@ def tile_routed_moe_kernel(tc, xT, w, b, gate, offs, pos1, pos2, out):
             nc.sync.dma_start(out=gate_block[:], in_=gate[:, n * P : (n + 1) * P, :].rearrange("r p t -> p r t"))
             gates.append(gate_block)
 
+        firsts, seconds = [], []
         for n in range(BLOCKS):
             first = ring.tile([P, T], F32, name="first", tag="first", bufs=BLOCKS)
             second = ring.tile([P, T], F32, name="second", tag="second", bufs=BLOCKS)
             nc.vector.tensor_tensor(out=first[:], in0=y[n][:].indirect(pos1_list[:]), in1=gates[n][:, 0, :], op=MULT)
-            nc.vector.tensor_tensor(out=second[:], in0=y[n][:].indirect(pos2_list[:]), in1=gates[n][:, 1, :], op=MULT)
+            nc.scalar.activation(out=second[:], in_=y[n][:].indirect(pos2_list[:]), func=COPY)
+            firsts.append(first)
+            seconds.append(second)
+        for n in range(BLOCKS):
+            weighted = ring.tile([P, T], F32, name="weighted", tag="weighted", bufs=BLOCKS)
             result = ring.tile([P, T], F32, name="result", tag="result", bufs=BLOCKS)
-            if n == 0:
-                total = psum.tile([P, T], F32, name="total", tag="bank")
-                nc.tensor.matmul(total[:], identity[:], first[:], start=True, stop=False)
-                nc.tensor.matmul(total[:], identity[:], second[:], start=False, stop=True)
-                nc.scalar.copy(out=result[:], in_=total[:])
-            else:
-                nc.vector.tensor_tensor(out=result[:], in0=first[:], in1=second[:], op=ADD)
+            halves = ((0, T // 2), (T // 2, T))
+            for lo, hi in halves:
+                nc.vector.tensor_tensor(
+                    out=weighted[:, lo:hi], in0=seconds[n][:, lo:hi], in1=gates[n][:, 1, lo:hi], op=MULT
+                )
+            for lo, hi in halves:
+                nc.vector.tensor_tensor(out=result[:, lo:hi], in0=firsts[n][:, lo:hi], in1=weighted[:, lo:hi], op=ADD)
             nc.sync.dma_start(out=out[n * P : (n + 1) * P, :], in_=result[:])

@@ -31,12 +31,14 @@ PLANES_PER_TILE = 4
 SLOT_SLICES = {1: ((0, 384), (384, 768), (768, 1024)), 2: ((0, 768), (768, 1024)), 3: ((0, 1024),)}
 
 SCALAR_ALONE_UNITS = 8
-VECTOR_ALONE_UNITS = (10, 11, 12, 15, 16)
+VECTOR_ALONE_UNITS = (12, 13, 15, 16)
 SHARED = 0.4
 
-RAW_BUFS = 12
-GROUPED_BUFS = 5
-CODE_BUFS = 12
+BIAS_UNIT = 11
+GPSIMD_UNITS = 6
+RAW_BUFS = 13
+GROUPED_BUFS = 10
+CODE_BUFS = 10
 
 
 def interleave(nc, grouped, raw, scalar_share):
@@ -63,7 +65,6 @@ def tile_routed_moe_kernel(tc, xT, w, b, gate, offs, pos1, pos2, out):
         offs_list = keep.tile([P, SLOTS // LIST_ROWS], U16, name="offs_list")
         pos1_list = keep.tile([P, T // LIST_ROWS], U16, name="pos1_list")
         pos2_list = keep.tile([P, T // LIST_ROWS], U16, name="pos2_list")
-        bias = keep.tile([P, BLOCKS, E], F32, name="bias")
 
         token_codes = keep.tile([P, PASSES * T], U32, name="token_codes", align_bytes=64)
         token_scales = keep.tile([P, 2 * T], U8, name="token_scales", align_bytes=64)
@@ -80,7 +81,6 @@ def tile_routed_moe_kernel(tc, xT, w, b, gate, offs, pos1, pos2, out):
             x_raw.append(raw)
             if a == 0:
                 nc.sync.dma_start(out=offs_list[:], in_=offs)
-        nc.sync.dma_start(out=bias[:], in_=b.rearrange("(n p) e -> p n e", p=P))
 
         def gather(dst, tokens, start, width):
             for lo, hi in SLOT_SLICES[width]:
@@ -124,7 +124,7 @@ def tile_routed_moe_kernel(tc, xT, w, b, gate, offs, pos1, pos2, out):
             y_block = keep.tile([P, SLOTS], F32, name=f"y{n}")
             y.append(y_block)
 
-        def relu(engine, sums, e, n):
+        def relu(engine, bias, sums, e, n):
             part = y[n][:, e * C : (e + 1) * C]
             if engine == "scalar":
                 nc.scalar.activation(out=part, in_=sums, func=RELU, bias=bias[:, n, e : e + 1])
@@ -154,10 +154,21 @@ def tile_routed_moe_kernel(tc, xT, w, b, gate, offs, pos1, pos2, out):
             codes = ring.tile([P, N], U32, name="w_codes", tag="w_codes", bufs=CODE_BUFS, align_bytes=64)
             scales = ring.tile([P, N], U8, name="w_scales", tag="w_scales", bufs=CODE_BUFS, align_bytes=64)
             if not last:
-                share = 1 if unit < SCALAR_ALONE_UNITS else 0 if unit in VECTOR_ALONE_UNITS else SHARED
+                share = 1 if unit < SCALAR_ALONE_UNITS else 0 if unit in VECTOR_ALONE_UNITS else 0.5
                 pieces = ((0, 2 * P), (2 * P, N)) if share == 0 else ((0, N),)
-                for lo, hi in pieces:
-                    interleave(nc, grouped[:, PACK * lo : PACK * hi], raw[:, :, lo:hi], share)
+                if unit < GPSIMD_UNITS:
+                    interleave(nc, grouped[:, : PACK * 2 * P], raw[:, :, : 2 * P], share)
+                    nc.gpsimd.tensor_scalar(
+                        out=grouped[:, PACK * 2 * P :].rearrange("p (c t) -> p c t", t=PACK),
+                        in0=raw[:, :, 2 * P :].rearrange("p t c -> p c t"),
+                        scalar1=1.0,
+                        scalar2=0.0,
+                        op0=MULT,
+                        op1=ADD,
+                    )
+                else:
+                    for lo, hi in pieces:
+                        interleave(nc, grouped[:, PACK * lo : PACK * hi], raw[:, :, lo:hi], share)
                 for lo, hi in pieces:
                     nc.vector.quantize_mx(
                         out=codes[:, lo:hi].bitcast(FP8X4), scales=scales[:, lo:hi], in_=grouped[:, PACK * lo : PACK * hi]
@@ -177,16 +188,19 @@ def tile_routed_moe_kernel(tc, xT, w, b, gate, offs, pos1, pos2, out):
                     sums[(e, n)] = bank[:]
                 features = slice(n * P, (n + 1) * P)
                 multiply(sums[(e, n)], e, a, codes[:, features], scales[:, features])
-            if a == PASSES - 1 and e in (1, 2):
-                first_expert = 0 if e == 1 else e
+            if unit == BIAS_UNIT:
+                bias = ring.tile([P, BLOCKS, E], F32, name="bias", tag="raw", bufs=RAW_BUFS)
+                nc.sync.dma_start(out=bias[:], in_=b.rearrange("(n p) e -> p n e", p=P))
+            if unit == BIAS_UNIT or (e, a) == (2, PASSES - 1):
+                first_expert, last_expert = (0, 1) if unit == BIAS_UNIT else (e, e)
                 for n in range(BLOCKS):
-                    for done in range(first_expert, e + 1):
-                        relu("scalar", sums[(done, n)], done, n)
+                    for done in range(first_expert, last_expert + 1):
+                        relu("scalar", bias, sums[(done, n)], done, n)
                 for n in range(BLOCKS):
-                    square("scalar", first_expert, e, n)
+                    square("scalar", first_expert, last_expert, n)
             if last:
                 for n in range(BLOCKS):
-                    relu("vector", sums[(e, n)], e, n)
+                    relu("vector", bias, sums[(e, n)], e, n)
                     square("scalar", e, e, n)
 
         nc.sync.dma_start(out=pos1_list[:], in_=pos1)
@@ -206,8 +220,7 @@ def tile_routed_moe_kernel(tc, xT, w, b, gate, offs, pos1, pos2, out):
             firsts.append(first)
             seconds.append(second)
         for n in range(BLOCKS):
-            weighted = ring.tile([P, T], F32, name="weighted", tag="weighted", bufs=BLOCKS)
-            result = ring.tile([P, T], F32, name="result", tag="result", bufs=BLOCKS)
+            weighted, result = seconds[n], firsts[n]
             halves = ((0, T // 2), (T // 2, T))
             for lo, hi in halves:
                 nc.vector.tensor_tensor(

@@ -211,21 +211,37 @@ def tile_routed_moe_kernel(tc, xT, w, b, gate, offs, pos1, pos2, out):
             nc.sync.dma_start(out=gate_block[:], in_=gate[:, n * P : (n + 1) * P, :].rearrange("r p t -> p r t"))
             gates.append(gate_block)
 
-        firsts, seconds = [], []
+        halves = ((0, T // 2), (T // 2, T))
+        fetched = []
         for n in range(BLOCKS):
-            first = ring.tile([P, T], F32, name="first", tag="first", bufs=BLOCKS)
-            second = ring.tile([P, T], F32, name="second", tag="second", bufs=BLOCKS)
-            nc.vector.tensor_tensor(out=first[:], in0=y[n][:].indirect(pos1_list[:]), in1=gates[n][:, 0, :], op=MULT)
-            nc.scalar.activation(out=second[:], in_=y[n][:].indirect(pos2_list[:]), func=COPY)
-            firsts.append(first)
-            seconds.append(second)
-        for n in range(BLOCKS):
-            weighted, result = seconds[n], firsts[n]
-            halves = ((0, T // 2), (T // 2, T))
-            for lo, hi in halves:
-                nc.vector.tensor_tensor(
-                    out=weighted[:, lo:hi], in0=seconds[n][:, lo:hi], in1=gates[n][:, 1, lo:hi], op=MULT
-                )
-            for lo, hi in halves:
-                nc.vector.tensor_tensor(out=result[:, lo:hi], in0=firsts[n][:, lo:hi], in1=weighted[:, lo:hi], op=ADD)
-            nc.sync.dma_start(out=out[n * P : (n + 1) * P, :], in_=result[:])
+            both = ring.tile([P, 2, T], F32, name="fetched", tag="fetched", bufs=BLOCKS)
+            fetched.append(both)
+        last_block = BLOCKS - 1
+        for n in range(last_block):
+            nc.vector.tensor_tensor(
+                out=fetched[n][:, 0, :], in0=y[n][:].indirect(pos1_list[:]), in1=gates[n][:, 0, :], op=MULT
+            )
+            nc.scalar.activation(out=fetched[n][:, 1, :], in_=y[n][:].indirect(pos2_list[:]), func=COPY)
+        nc.scalar.activation(out=fetched[last_block][:, 0, :], in_=y[last_block][:].indirect(pos1_list[:]), func=COPY)
+        for lo, hi in halves:
+            offsets = pos2_list[:, lo // LIST_ROWS : hi // LIST_ROWS]
+            nc.scalar.activation(out=fetched[last_block][:, 1, lo:hi], in_=y[last_block][:].indirect(offsets), func=COPY)
+
+        def weight(n, r, lo, hi):
+            part = fetched[n][:, r, lo:hi]
+            nc.vector.tensor_tensor(out=part, in0=part, in1=gates[n][:, r, lo:hi], op=MULT)
+
+        def add_and_store(n, lo, hi):
+            part = fetched[n][:, 0, lo:hi]
+            nc.vector.tensor_tensor(out=part, in0=part, in1=fetched[n][:, 1, lo:hi], op=ADD)
+            nc.sync.dma_start(out=out[n * P : (n + 1) * P, lo:hi], in_=part)
+
+        for n in range(last_block):
+            weight(n, 1, 0, T)
+        for n in range(last_block):
+            add_and_store(n, 0, T)
+        weight(last_block, 0, 0, T)
+        for lo, hi in halves:
+            weight(last_block, 1, lo, hi)
+        for lo, hi in halves:
+            add_and_store(last_block, lo, hi)

@@ -36,6 +36,9 @@ SHARED = 0.4
 
 BIAS_UNIT = 11
 GPSIMD_UNITS = 6
+LATE_PASSES = 2
+WHOLE_UNITS = UNITS - LATE_PASSES
+LATE_SHARES = ((1, 0), (1, 0), (1, 0))
 RAW_BUFS = 13
 GROUPED_BUFS = 10
 CODE_BUFS = 10
@@ -145,43 +148,32 @@ def tile_routed_moe_kernel(tc, xT, w, b, gate, offs, pos1, pos2, out):
             pair = psum.tile([P, 2 * C], F32, name="pair", tag="bank")
             sums[(0, n)] = pair[:, 0:C]
             sums[(1, n)] = pair[:, C : 2 * C]
-        for unit in range(UNITS):
+        for unit in range(WHOLE_UNITS):
             e, a = unit // PASSES, unit % PASSES
-            last = unit == UNITS - 1
             raw = ring.tile([P, PACK, N], F32, name="w_raw", tag="raw", bufs=RAW_BUFS)
             nc.sync.dma_start(out=raw[:], in_=w_rows[e, a])
             grouped = ring.tile([P, N * PACK], BF16, name="w_grouped", tag="grouped", bufs=GROUPED_BUFS, align_bytes=64)
             codes = ring.tile([P, N], U32, name="w_codes", tag="w_codes", bufs=CODE_BUFS, align_bytes=64)
             scales = ring.tile([P, N], U8, name="w_scales", tag="w_scales", bufs=CODE_BUFS, align_bytes=64)
-            if not last:
-                share = 1 if unit < SCALAR_ALONE_UNITS else 0 if unit in VECTOR_ALONE_UNITS else 0.5
-                pieces = ((0, 2 * P), (2 * P, N)) if share == 0 else ((0, N),)
-                if unit < GPSIMD_UNITS:
-                    interleave(nc, grouped[:, : PACK * 2 * P], raw[:, :, : 2 * P], share)
-                    nc.gpsimd.tensor_scalar(
-                        out=grouped[:, PACK * 2 * P :].rearrange("p (c t) -> p c t", t=PACK),
-                        in0=raw[:, :, 2 * P :].rearrange("p t c -> p c t"),
-                        scalar1=1.0,
-                        scalar2=0.0,
-                        op0=MULT,
-                        op1=ADD,
-                    )
-                else:
-                    for lo, hi in pieces:
-                        interleave(nc, grouped[:, PACK * lo : PACK * hi], raw[:, :, lo:hi], share)
-                for lo, hi in pieces:
-                    nc.vector.quantize_mx(
-                        out=codes[:, lo:hi].bitcast(FP8X4), scales=scales[:, lo:hi], in_=grouped[:, PACK * lo : PACK * hi]
-                    )
+            share = 1 if unit < SCALAR_ALONE_UNITS else 0 if unit in VECTOR_ALONE_UNITS else 0.5
+            pieces = ((0, 2 * P), (2 * P, N)) if share == 0 else ((0, N),)
+            if unit < GPSIMD_UNITS:
+                interleave(nc, grouped[:, : PACK * 2 * P], raw[:, :, : 2 * P], share)
+                nc.gpsimd.tensor_scalar(
+                    out=grouped[:, PACK * 2 * P :].rearrange("p (c t) -> p c t", t=PACK),
+                    in0=raw[:, :, 2 * P :].rearrange("p t c -> p c t"),
+                    scalar1=1.0,
+                    scalar2=0.0,
+                    op0=MULT,
+                    op1=ADD,
+                )
             else:
-                for n, share in ((0, 0), (1, 1), (2, 0)):
-                    interleave(nc, grouped[:, PACK * n * P : PACK * (n + 1) * P], raw[:, :, n * P : (n + 1) * P], share)
-                for n in range(BLOCKS):
-                    nc.vector.quantize_mx(
-                        out=codes[:, n * P : (n + 1) * P].bitcast(FP8X4),
-                        scales=scales[:, n * P : (n + 1) * P],
-                        in_=grouped[:, PACK * n * P : PACK * (n + 1) * P],
-                    )
+                for lo, hi in pieces:
+                    interleave(nc, grouped[:, PACK * lo : PACK * hi], raw[:, :, lo:hi], share)
+            for lo, hi in pieces:
+                nc.vector.quantize_mx(
+                    out=codes[:, lo:hi].bitcast(FP8X4), scales=scales[:, lo:hi], in_=grouped[:, PACK * lo : PACK * hi]
+                )
             for n in range(BLOCKS):
                 if a == 0 and e > 1:
                     bank = psum.tile([P, C], F32, name="bank", tag="bank")
@@ -198,18 +190,35 @@ def tile_routed_moe_kernel(tc, xT, w, b, gate, offs, pos1, pos2, out):
                         relu("scalar", bias, sums[(done, n)], done, n)
                 for n in range(BLOCKS):
                     square("scalar", first_expert, last_expert, n)
-            if last:
-                for n in range(BLOCKS):
-                    relu("vector", bias, sums[(e, n)], e, n)
-                    square("scalar", e, e, n)
 
-        nc.sync.dma_start(out=pos1_list[:], in_=pos1)
-        nc.sync.dma_start(out=pos2_list[:], in_=pos2)
-        gates = []
-        for n in range(BLOCKS):
+        def load_gates(n):
             gate_block = ring.tile([P, 2, T], F32, name="gate_block", tag="raw", bufs=RAW_BUFS)
             nc.sync.dma_start(out=gate_block[:], in_=gate[:, n * P : (n + 1) * P, :].rearrange("r p t -> p r t"))
-            gates.append(gate_block)
+            return gate_block
+
+        e = E - 1
+        late = range(PASSES - LATE_PASSES, PASSES)
+        gates = {}
+        for n in range(BLOCKS):
+            grouped = ring.tile([P, LATE_PASSES * P * PACK], BF16, name="w_grouped", tag="grouped", bufs=GROUPED_BUFS, align_bytes=64)
+            codes = ring.tile([P, LATE_PASSES * P], U32, name="w_codes", tag="w_codes", bufs=CODE_BUFS, align_bytes=64)
+            scales = ring.tile([P, LATE_PASSES * P], U8, name="w_scales", tag="w_scales", bufs=CODE_BUFS, align_bytes=64)
+            for i, a in enumerate(late):
+                raw = ring.tile([P, PACK, P], F32, name="w_late", tag="raw", bufs=RAW_BUFS)
+                nc.sync.dma_start(out=raw[:], in_=w_rows[e, a, :, :, n * P : (n + 1) * P])
+                interleave(nc, grouped[:, i * P * PACK : (i + 1) * P * PACK], raw[:], LATE_SHARES[n][i])
+            for lo, hi in ((0, (LATE_PASSES - 1) * P), ((LATE_PASSES - 1) * P, LATE_PASSES * P)):
+                nc.vector.quantize_mx(
+                    out=codes[:, lo:hi].bitcast(FP8X4), scales=scales[:, lo:hi], in_=grouped[:, PACK * lo : PACK * hi]
+                )
+            for i, a in enumerate(late):
+                multiply(sums[(e, n)], e, a, codes[:, i * P : (i + 1) * P], scales[:, i * P : (i + 1) * P])
+            relu("scalar", bias, sums[(e, n)], e, n)
+            square("scalar", e, e, n)
+        nc.sync.dma_start(out=pos2_list[:], in_=pos2)
+        nc.sync.dma_start(out=pos1_list[:], in_=pos1)
+        for n in range(BLOCKS):
+            gates[n] = load_gates(n)
 
         halves = ((0, T // 2), (T // 2, T))
         fetched = []

@@ -35,7 +35,7 @@ VECTOR_ALONE_UNITS = (12, 13, 15, 16)
 SHARED = 0.4
 
 BIAS_UNIT = 11
-GPSIMD_UNITS = 6
+GPSIMD_UNITS = 0
 LATE_PASSES = 2
 WHOLE_UNITS = UNITS - LATE_PASSES
 LATE_SHARES = ((1, 0), (1, 0), (1, 0))

@@ -35,10 +35,7 @@ VECTOR_ALONE_UNITS = (12, 13, 15, 16)
 SHARED = 0.4
 
 BIAS_UNIT = 11
-GPSIMD_UNITS = 0
-LATE_PASSES = 2
-WHOLE_UNITS = UNITS - LATE_PASSES
-LATE_SHARES = ((1, 0), (1, 0), (1, 0))
+WHOLE_UNITS = UNITS - 1
 RAW_BUFS = 13
 GROUPED_BUFS = 10
 CODE_BUFS = 10
@@ -155,22 +152,17 @@ def tile_routed_moe_kernel(tc, xT, w, b, gate, offs, pos1, pos2, out):
             grouped = ring.tile([P, N * PACK], BF16, name="w_grouped", tag="grouped", bufs=GROUPED_BUFS, align_bytes=64)
             codes = ring.tile([P, N], U32, name="w_codes", tag="w_codes", bufs=CODE_BUFS, align_bytes=64)
             scales = ring.tile([P, N], U8, name="w_scales", tag="w_scales", bufs=CODE_BUFS, align_bytes=64)
-            share = 1 if unit < SCALAR_ALONE_UNITS else 0 if unit in VECTOR_ALONE_UNITS else 0.5
-            pieces = ((0, 2 * P), (2 * P, N)) if share == 0 else ((0, N),)
-            if unit < GPSIMD_UNITS:
-                interleave(nc, grouped[:, : PACK * 2 * P], raw[:, :, : 2 * P], share)
-                nc.gpsimd.tensor_scalar(
-                    out=grouped[:, PACK * 2 * P :].rearrange("p (c t) -> p c t", t=PACK),
-                    in0=raw[:, :, 2 * P :].rearrange("p t c -> p c t"),
-                    scalar1=1.0,
-                    scalar2=0.0,
-                    op0=MULT,
-                    op1=ADD,
-                )
+            if unit < SCALAR_ALONE_UNITS:
+                pieces = ((0, N, 1),)
+            elif unit in VECTOR_ALONE_UNITS:
+                pieces = ((0, 2 * P, 0), (2 * P, N, 0))
+            elif unit == WHOLE_UNITS - 1:
+                pieces = ((0, P, 0), (P, N, 1))
             else:
-                for lo, hi in pieces:
-                    interleave(nc, grouped[:, PACK * lo : PACK * hi], raw[:, :, lo:hi], share)
-            for lo, hi in pieces:
+                pieces = ((0, N, 0.5),)
+            for lo, hi, share in pieces:
+                interleave(nc, grouped[:, PACK * lo : PACK * hi], raw[:, :, lo:hi], share)
+            for lo, hi, share in pieces:
                 nc.vector.quantize_mx(
                     out=codes[:, lo:hi].bitcast(FP8X4), scales=scales[:, lo:hi], in_=grouped[:, PACK * lo : PACK * hi]
                 )
@@ -196,25 +188,29 @@ def tile_routed_moe_kernel(tc, xT, w, b, gate, offs, pos1, pos2, out):
             nc.sync.dma_start(out=gate_block[:], in_=gate[:, n * P : (n + 1) * P, :].rearrange("r p t -> p r t"))
             return gate_block
 
-        e = E - 1
-        late = range(PASSES - LATE_PASSES, PASSES)
+        e, a = E - 1, PASSES - 1
         gates = {}
-        for n in range(BLOCKS):
-            grouped = ring.tile([P, LATE_PASSES * P * PACK], BF16, name="w_grouped", tag="grouped", bufs=GROUPED_BUFS, align_bytes=64)
-            codes = ring.tile([P, LATE_PASSES * P], U32, name="w_codes", tag="w_codes", bufs=CODE_BUFS, align_bytes=64)
-            scales = ring.tile([P, LATE_PASSES * P], U8, name="w_scales", tag="w_scales", bufs=CODE_BUFS, align_bytes=64)
-            for i, a in enumerate(late):
-                raw = ring.tile([P, PACK, P], F32, name="w_late", tag="raw", bufs=RAW_BUFS)
-                nc.sync.dma_start(out=raw[:], in_=w_rows[e, a, :, :, n * P : (n + 1) * P])
-                interleave(nc, grouped[:, i * P * PACK : (i + 1) * P * PACK], raw[:], LATE_SHARES[n][i])
-            for lo, hi in ((0, (LATE_PASSES - 1) * P), ((LATE_PASSES - 1) * P, LATE_PASSES * P)):
+        grouped = ring.tile([P, N * PACK], BF16, name="w_grouped", tag="grouped", bufs=GROUPED_BUFS, align_bytes=64)
+        codes = ring.tile([P, N], U32, name="w_codes", tag="w_codes", bufs=CODE_BUFS, align_bytes=64)
+        scales = ring.tile([P, N], U8, name="w_scales", tag="w_scales", bufs=CODE_BUFS, align_bytes=64)
+        for blocks, share in (((0,), 0), ((1, 2), 0)):
+            first = blocks[0] * P
+            raw = ring.tile([P, PACK, len(blocks) * P], F32, name="w_late", tag="raw", bufs=RAW_BUFS)
+            nc.sync.dma_start(out=raw[:], in_=w_rows[e, a, :, :, first : first + len(blocks) * P])
+            for n in blocks:
+                interleave(nc, grouped[:, PACK * n * P : PACK * (n + 1) * P], raw[:, :, n * P - first : (n + 1) * P - first], share)
+            for n in blocks:
+                features = slice(n * P, (n + 1) * P)
                 nc.vector.quantize_mx(
-                    out=codes[:, lo:hi].bitcast(FP8X4), scales=scales[:, lo:hi], in_=grouped[:, PACK * lo : PACK * hi]
+                    out=codes[:, features].bitcast(FP8X4),
+                    scales=scales[:, features],
+                    in_=grouped[:, PACK * n * P : PACK * (n + 1) * P],
                 )
-            for i, a in enumerate(late):
-                multiply(sums[(e, n)], e, a, codes[:, i * P : (i + 1) * P], scales[:, i * P : (i + 1) * P])
-            relu("scalar", bias, sums[(e, n)], e, n)
-            square("scalar", e, e, n)
+                multiply(sums[(e, n)], e, a, codes[:, features], scales[:, features])
+            for n in blocks:
+                relu("vector" if n == 1 else "scalar", bias, sums[(e, n)], e, n)
+            for n in blocks:
+                square("scalar", e, e, n)
         nc.sync.dma_start(out=pos2_list[:], in_=pos2)
         nc.sync.dma_start(out=pos1_list[:], in_=pos1)
         for n in range(BLOCKS):

@@ -30,13 +30,15 @@ FLOPS = 2 * K * N * E * C
 PLANES_PER_TILE = 4
 SLOT_SLICES = {1: ((0, 384), (384, 768), (768, 1024)), 2: ((0, 768), (768, 1024)), 3: ((0, 1024),)}
 
-SCALAR_ALONE_UNITS = 8
-VECTOR_ALONE_UNITS = (12, 13, 15, 16)
 SHARED = 0.4
 
-BIAS_UNIT = 11
+LOADS = ((0,), (1, 2, 3), (4, 5, 6), (7, 8, 9), (10, 11, 12), (13, 14), (15,), (16,), (17,), (18,))
+SCALAR_UNITS = (0, 1, 2, 3, 4, 5, 8, 12, 13)
+HALVED_UNITS = (9, 17)
+BIAS_UNIT = 9
 WHOLE_UNITS = UNITS - 1
-RAW_BUFS = 13
+RAW_BUFS = 7
+GROUP_BUFS = 3
 GROUPED_BUFS = 10
 CODE_BUFS = 10
 
@@ -61,6 +63,7 @@ def tile_routed_moe_kernel(tc, xT, w, b, gate, offs, pos1, pos2, out):
 
         x_rows = xT.rearrange("(a p j) t -> a p j t", p=P, j=PACK)
         w_rows = w.rearrange("e (a p j) n -> e a p j n", p=P, j=PACK)
+        w_units = w.rearrange("e (a p j) n -> p (e a) j n", p=P, j=PACK)
 
         offs_list = keep.tile([P, SLOTS // LIST_ROWS], U16, name="offs_list")
         pos1_list = keep.tile([P, T // LIST_ROWS], U16, name="pos1_list")
@@ -74,8 +77,21 @@ def tile_routed_moe_kernel(tc, xT, w, b, gate, offs, pos1, pos2, out):
             slots = keep.tile([P, SLOTS], U8, name=f"slot_scales{i}", align_bytes=64)
             slot_scales.append(slots)
 
+        w_raw = {}
+
+        def load_units(units):
+            if len(units) == 1:
+                raw = ring.tile([P, 1, PACK, N], F32, name="w_single", tag="raw", bufs=RAW_BUFS)
+            else:
+                raw = ring.tile([P, len(units), PACK, N], F32, name="w_group", tag="group", bufs=GROUP_BUFS)
+            nc.sync.dma_start(out=raw[:], in_=w_units[:, units[0] : units[-1] + 1])
+            for i, unit in enumerate(units):
+                w_raw[unit] = raw[:, i]
+
         x_raw = []
         for a in range(PASSES):
+            if a == PASSES - 1:
+                load_units(LOADS[0])
             raw = ring.tile([P, PACK, T], F32, name="x_raw", tag="raw", bufs=RAW_BUFS)
             nc.sync.dma_start(out=raw[:], in_=x_rows[a])
             x_raw.append(raw)
@@ -140,48 +156,56 @@ def tile_routed_moe_kernel(tc, xT, w, b, gate, offs, pos1, pos2, out):
             else:
                 nc.vector.tensor_tensor(out=part, in0=part, in1=part, op=MULT)
 
+        def pieces_of(unit):
+            if unit in SCALAR_UNITS:
+                return ((0, N, 1),)
+            if unit == WHOLE_UNITS - 1:
+                return ((0, P, 0), (P, N, 1))
+            if unit in HALVED_UNITS:
+                return ((0, N, 0.5),)
+            if unit >= LOADS[6][0]:
+                return ((0, 2 * P, 0), (2 * P, N, 0))
+            return ((0, N, 0),)
+
         sums = {}
-        for n in range(BLOCKS):
-            pair = psum.tile([P, 2 * C], F32, name="pair", tag="bank")
-            sums[(0, n)] = pair[:, 0:C]
-            sums[(1, n)] = pair[:, C : 2 * C]
-        for unit in range(WHOLE_UNITS):
-            e, a = unit // PASSES, unit % PASSES
-            raw = ring.tile([P, PACK, N], F32, name="w_raw", tag="raw", bufs=RAW_BUFS)
-            nc.sync.dma_start(out=raw[:], in_=w_rows[e, a])
-            grouped = ring.tile([P, N * PACK], BF16, name="w_grouped", tag="grouped", bufs=GROUPED_BUFS, align_bytes=64)
-            codes = ring.tile([P, N], U32, name="w_codes", tag="w_codes", bufs=CODE_BUFS, align_bytes=64)
-            scales = ring.tile([P, N], U8, name="w_scales", tag="w_scales", bufs=CODE_BUFS, align_bytes=64)
-            if unit < SCALAR_ALONE_UNITS:
-                pieces = ((0, N, 1),)
-            elif unit in VECTOR_ALONE_UNITS:
-                pieces = ((0, 2 * P, 0), (2 * P, N, 0))
-            elif unit == WHOLE_UNITS - 1:
-                pieces = ((0, P, 0), (P, N, 1))
-            else:
-                pieces = ((0, N, 0.5),)
-            for lo, hi, share in pieces:
-                interleave(nc, grouped[:, PACK * lo : PACK * hi], raw[:, :, lo:hi], share)
-            for lo, hi, share in pieces:
-                nc.vector.quantize_mx(
-                    out=codes[:, lo:hi].bitcast(FP8X4), scales=scales[:, lo:hi], in_=grouped[:, PACK * lo : PACK * hi]
-                )
-            for n in range(BLOCKS):
-                if a == 0 and e > 1:
-                    bank = psum.tile([P, C], F32, name="bank", tag="bank")
-                    sums[(e, n)] = bank[:]
-                features = slice(n * P, (n + 1) * P)
-                multiply(sums[(e, n)], e, a, codes[:, features], scales[:, features])
-            if unit == BIAS_UNIT:
-                bias = ring.tile([P, BLOCKS, E], F32, name="bias", tag="raw", bufs=RAW_BUFS)
+        closed = []
+        for units in LOADS:
+            if units[0] > 0:
+                load_units(units)
+            if BIAS_UNIT in units:
+                bias = keep.tile([P, BLOCKS, E], F32, name="bias")
                 nc.sync.dma_start(out=bias[:], in_=b.rearrange("(n p) e -> p n e", p=P))
-            if unit == BIAS_UNIT or (e, a) == (2, PASSES - 1):
-                first_expert, last_expert = (0, 1) if unit == BIAS_UNIT else (e, e)
+            grouped = {}
+            for unit in units:
+                tile = ring.tile([P, N * PACK], BF16, name="w_grouped", tag="grouped", bufs=GROUPED_BUFS, align_bytes=64)
+                grouped[unit] = tile
+                for lo, hi, share in pieces_of(unit):
+                    interleave(nc, tile[:, PACK * lo : PACK * hi], w_raw[unit][:, :, lo:hi], share)
+            for unit in units:
+                e, a = unit // PASSES, unit % PASSES
+                codes = ring.tile([P, N], U32, name="w_codes", tag="w_codes", bufs=CODE_BUFS, align_bytes=64)
+                scales = ring.tile([P, N], U8, name="w_scales", tag="w_scales", bufs=CODE_BUFS, align_bytes=64)
+                for lo, hi, share in pieces_of(unit):
+                    nc.vector.quantize_mx(
+                        out=codes[:, lo:hi].bitcast(FP8X4),
+                        scales=scales[:, lo:hi],
+                        in_=grouped[unit][:, PACK * lo : PACK * hi],
+                    )
                 for n in range(BLOCKS):
-                    for done in range(first_expert, last_expert + 1):
-                        relu("scalar", bias, sums[(done, n)], done, n)
+                    if a == 0:
+                        bank = psum.tile([P, C], F32, name="bank", tag="bank")
+                        sums[(e, n)] = bank[:]
+                    features = slice(n * P, (n + 1) * P)
+                    multiply(sums[(e, n)], e, a, codes[:, features], scales[:, features])
+                if a == PASSES - 1:
+                    closed.append(e)
+            if closed and units[-1] >= BIAS_UNIT:
+                for e in closed:
+                    for n in range(BLOCKS):
+                        relu("scalar", bias, sums[(e, n)], e, n)
                 for n in range(BLOCKS):
-                    square("scalar", first_expert, last_expert, n)
+                    square("scalar", closed[0], closed[-1], n)
+                closed.clear()
 
         def load_gates(n):
             gate_block = ring.tile([P, 2, T], F32, name="gate_block", tag="raw", bufs=RAW_BUFS)

@@ -32,10 +32,10 @@ SLOT_SLICES = {1: ((0, 384), (384, 768), (768, 1024)), 2: ((0, 768), (768, 1024)
 
 SHARED = 0.4
 
-LOADS = ((0,), (1, 2, 3), (4, 5, 6), (7, 8, 9), (10, 11, 12), (13, 14), (15,), (16,), (17,), (18,))
-SCALAR_UNITS = (0, 1, 2, 3, 4, 5, 8, 12, 13)
-HALVED_UNITS = (9, 17)
-BIAS_UNIT = 9
+LOADS = ((0,), (1, 2), (3, 4, 5), (6, 7, 8), (9, 10, 11), (12, 13), (14,), (15,), (16,), (17,), (18,))
+SCALAR_UNITS = (0, 1, 2, 3, 4, 5, 6, 10, 14)
+HALVED_UNITS = (11, 15, 17)
+BIAS_UNIT = 8
 WHOLE_UNITS = UNITS - 1
 RAW_BUFS = 7
 GROUP_BUFS = 3
@@ -163,12 +163,21 @@ def tile_routed_moe_kernel(tc, xT, w, b, gate, offs, pos1, pos2, out):
                 return ((0, P, 0), (P, N, 1))
             if unit in HALVED_UNITS:
                 return ((0, N, 0.5),)
-            if unit >= LOADS[6][0]:
+            if unit >= LOADS[7][0]:
                 return ((0, 2 * P, 0), (2 * P, N, 0))
             return ((0, N, 0),)
 
         sums = {}
         closed = []
+
+        def empty_banks():
+            for e in closed:
+                for n in range(BLOCKS):
+                    relu("scalar", bias, sums[(e, n)], e, n)
+            for n in range(BLOCKS):
+                square("scalar", closed[0], closed[-1], n)
+            closed.clear()
+
         for units in LOADS:
             if units[0] > 0:
                 load_units(units)
@@ -181,6 +190,8 @@ def tile_routed_moe_kernel(tc, xT, w, b, gate, offs, pos1, pos2, out):
                 grouped[unit] = tile
                 for lo, hi, share in pieces_of(unit):
                     interleave(nc, tile[:, PACK * lo : PACK * hi], w_raw[unit][:, :, lo:hi], share)
+            if units[0] == LOADS[7][0]:
+                empty_banks()
             for unit in units:
                 e, a = unit // PASSES, unit % PASSES
                 codes = ring.tile([P, N], U32, name="w_codes", tag="w_codes", bufs=CODE_BUFS, align_bytes=64)
@@ -199,13 +210,8 @@ def tile_routed_moe_kernel(tc, xT, w, b, gate, offs, pos1, pos2, out):
                     multiply(sums[(e, n)], e, a, codes[:, features], scales[:, features])
                 if a == PASSES - 1:
                     closed.append(e)
-            if closed and units[-1] >= BIAS_UNIT:
-                for e in closed:
-                    for n in range(BLOCKS):
-                        relu("scalar", bias, sums[(e, n)], e, n)
-                for n in range(BLOCKS):
-                    square("scalar", closed[0], closed[-1], n)
-                closed.clear()
+            if closed and closed[0] < E - 2 and units[-1] >= BIAS_UNIT:
+                empty_banks()
 
         def load_gates(n):
             gate_block = ring.tile([P, 2, T], F32, name="gate_block", tag="raw", bufs=RAW_BUFS)
@@ -231,6 +237,15 @@ def tile_routed_moe_kernel(tc, xT, w, b, gate, offs, pos1, pos2, out):
                     in_=grouped[:, PACK * n * P : PACK * (n + 1) * P],
                 )
                 multiply(sums[(e, n)], e, a, codes[:, features], scales[:, features])
+            if blocks == (0,):
+                for func in (RELU, SQUARE):
+                    for lo, hi in ((0, C // 2), (C // 2, C)):
+                        part = y[0][:, e * C + lo : e * C + hi]
+                        if func == RELU:
+                            nc.scalar.activation(out=part, in_=sums[(e, 0)][:, lo:hi], func=RELU, bias=bias[:, 0, e : e + 1])
+                        else:
+                            nc.scalar.activation(out=part, in_=part, func=SQUARE)
+                continue
             for n in blocks:
                 relu("vector" if n == 1 else "scalar", bias, sums[(e, n)], e, n)
             for n in blocks:

@@ -247,7 +247,7 @@ def tile_routed_moe_kernel(tc, xT, w, b, gate, offs, pos1, pos2, out):
                             nc.scalar.activation(out=part, in_=part, func=SQUARE)
                 continue
             for n in blocks:
-                relu("vector" if n == 1 else "scalar", bias, sums[(e, n)], e, n)
+                relu("scalar", bias, sums[(e, n)], e, n)
             for n in blocks:
                 square("scalar", e, e, n)
         nc.sync.dma_start(out=pos2_list[:], in_=pos2)

@@ -160,7 +160,7 @@ def tile_routed_moe_kernel(tc, xT, w, b, gate, offs, pos1, pos2, out):
             if unit in SCALAR_UNITS:
                 return ((0, N, 1),)
             if unit == WHOLE_UNITS - 1:
-                return ((0, P, 0), (P, N, 1))
+                return ((0, P, 1), (P, N, 0))
             if unit in HALVED_UNITS:
                 return ((0, N, 0.5),)
             if unit >= LOADS[7][0]:
@@ -213,63 +213,50 @@ def tile_routed_moe_kernel(tc, xT, w, b, gate, offs, pos1, pos2, out):
             if closed and closed[0] < E - 2 and units[-1] >= BIAS_UNIT:
                 empty_banks()
 
-        def load_gates(n):
-            gate_block = ring.tile([P, 2, T], F32, name="gate_block", tag="raw", bufs=RAW_BUFS)
-            nc.sync.dma_start(out=gate_block[:], in_=gate[:, n * P : (n + 1) * P, :].rearrange("r p t -> p r t"))
-            return gate_block
-
         e, a = E - 1, PASSES - 1
-        gates = {}
         grouped = ring.tile([P, N * PACK], BF16, name="w_grouped", tag="grouped", bufs=GROUPED_BUFS, align_bytes=64)
         codes = ring.tile([P, N], U32, name="w_codes", tag="w_codes", bufs=CODE_BUFS, align_bytes=64)
         scales = ring.tile([P, N], U8, name="w_scales", tag="w_scales", bufs=CODE_BUFS, align_bytes=64)
-        for blocks, share in (((0,), 0), ((1, 2), 0)):
-            first = blocks[0] * P
-            raw = ring.tile([P, PACK, len(blocks) * P], F32, name="w_late", tag="raw", bufs=RAW_BUFS)
-            nc.sync.dma_start(out=raw[:], in_=w_rows[e, a, :, :, first : first + len(blocks) * P])
-            for n in blocks:
-                interleave(nc, grouped[:, PACK * n * P : PACK * (n + 1) * P], raw[:, :, n * P - first : (n + 1) * P - first], share)
-            for n in blocks:
-                features = slice(n * P, (n + 1) * P)
-                nc.vector.quantize_mx(
-                    out=codes[:, features].bitcast(FP8X4),
-                    scales=scales[:, features],
-                    in_=grouped[:, PACK * n * P : PACK * (n + 1) * P],
-                )
-                multiply(sums[(e, n)], e, a, codes[:, features], scales[:, features])
-            if blocks == (0,):
-                for func in (RELU, SQUARE):
-                    for lo, hi in ((0, C // 2), (C // 2, C)):
-                        part = y[0][:, e * C + lo : e * C + hi]
-                        if func == RELU:
-                            nc.scalar.activation(out=part, in_=sums[(e, 0)][:, lo:hi], func=RELU, bias=bias[:, 0, e : e + 1])
-                        else:
-                            nc.scalar.activation(out=part, in_=part, func=SQUARE)
-                continue
-            for n in blocks:
-                relu("scalar", bias, sums[(e, n)], e, n)
-            for n in blocks:
-                square("scalar", e, e, n)
+        first = ring.tile([P, PACK, P], F32, name="w_first", tag="raw", bufs=RAW_BUFS)
+        nc.sync.dma_start(out=first[:], in_=w_rows[e, a, :, :, :P])
+        rest = ring.tile([P, PACK, N - P], F32, name="w_rest", tag="raw", bufs=RAW_BUFS)
+        nc.sync.dma_start(out=rest[:], in_=w_rows[e, a, :, :, P:])
         nc.sync.dma_start(out=pos2_list[:], in_=pos2)
         nc.sync.dma_start(out=pos1_list[:], in_=pos1)
+        gates = []
         for n in range(BLOCKS):
-            gates[n] = load_gates(n)
+            gate_block = ring.tile([P, 2, T], F32, name="gate_block", tag="raw", bufs=RAW_BUFS)
+            rows = gate[:, n * P : (n + 1) * P, :].rearrange("r p t -> p r t")
+            if n == 0:
+                for r in range(2):
+                    nc.sync.dma_start(out=gate_block[:, r, :], in_=rows[:, r, :])
+            else:
+                nc.sync.dma_start(out=gate_block[:], in_=rows)
+            gates.append(gate_block)
 
-        halves = ((0, T // 2), (T // 2, T))
         fetched = []
         for n in range(BLOCKS):
             both = ring.tile([P, 2, T], F32, name="fetched", tag="fetched", bufs=BLOCKS)
             fetched.append(both)
-        last_block = BLOCKS - 1
-        for n in range(last_block):
+        lists = (pos1_list, pos2_list)
+
+        def close_block(n):
+            features = slice(n * P, (n + 1) * P)
+            nc.vector.quantize_mx(
+                out=codes[:, features].bitcast(FP8X4),
+                scales=scales[:, features],
+                in_=grouped[:, PACK * n * P : PACK * (n + 1) * P],
+            )
+            multiply(sums[(e, n)], e, a, codes[:, features], scales[:, features])
+
+        def fetch(n, r, lo, hi):
+            offsets = lists[r][:, lo // LIST_ROWS : hi // LIST_ROWS]
+            nc.scalar.activation(out=fetched[n][:, r, lo:hi], in_=y[n][:].indirect(offsets), func=COPY)
+
+        def fetch_weighted(n):
             nc.vector.tensor_tensor(
                 out=fetched[n][:, 0, :], in0=y[n][:].indirect(pos1_list[:]), in1=gates[n][:, 0, :], op=MULT
             )
-            nc.scalar.activation(out=fetched[n][:, 1, :], in_=y[n][:].indirect(pos2_list[:]), func=COPY)
-        nc.scalar.activation(out=fetched[last_block][:, 0, :], in_=y[last_block][:].indirect(pos1_list[:]), func=COPY)
-        for lo, hi in halves:
-            offsets = pos2_list[:, lo // LIST_ROWS : hi // LIST_ROWS]
-            nc.scalar.activation(out=fetched[last_block][:, 1, lo:hi], in_=y[last_block][:].indirect(offsets), func=COPY)
 
         def weight(n, r, lo, hi):
             part = fetched[n][:, r, lo:hi]
@@ -280,12 +267,38 @@ def tile_routed_moe_kernel(tc, xT, w, b, gate, offs, pos1, pos2, out):
             nc.vector.tensor_tensor(out=part, in0=part, in1=fetched[n][:, 1, lo:hi], op=ADD)
             nc.sync.dma_start(out=out[n * P : (n + 1) * P, lo:hi], in_=part)
 
-        for n in range(last_block):
-            weight(n, 1, 0, T)
-        for n in range(last_block):
-            add_and_store(n, 0, T)
-        weight(last_block, 0, 0, T)
+        interleave(nc, grouped[:, : PACK * P], first[:], 1)
+        close_block(0)
+        for func in (RELU, SQUARE):
+            for lo, hi in ((0, C // 2), (C // 2, C)):
+                part = y[0][:, e * C + lo : e * C + hi]
+                if func == RELU:
+                    nc.scalar.activation(out=part, in_=sums[(e, 0)][:, lo:hi], func=RELU, bias=bias[:, 0, e : e + 1])
+                else:
+                    nc.scalar.activation(out=part, in_=part, func=SQUARE)
+        fetch(0, 1, 0, T)
+        for n in (1, 2):
+            interleave(nc, grouped[:, PACK * n * P : PACK * (n + 1) * P], rest[:, :, (n - 1) * P : n * P], 0)
+        for n in (1, 2):
+            close_block(n)
+        for n in (1, 2):
+            relu("scalar", bias, sums[(e, n)], e, n)
+        for n in (1, 2):
+            square("scalar", e, e, n)
+
+        halves = ((0, T // 2), (T // 2, T))
+        fetch_weighted(0)
+        weight(0, 1, 0, T)
+        fetch(1, 1, 0, T)
+        fetch_weighted(1)
+        add_and_store(0, 0, T)
+        weight(1, 1, 0, T)
+        fetch(2, 0, 0, T)
+        weight(2, 0, 0, T)
+        add_and_store(1, 0, T)
         for lo, hi in halves:
-            weight(last_block, 1, lo, hi)
+            fetch(2, 1, lo, hi)
         for lo, hi in halves:
-            add_and_store(last_block, lo, hi)
+            weight(2, 1, lo, hi)
+        for lo, hi in halves:
+            add_and_store(2, lo, hi)

@@ -7,6 +7,7 @@ K, T, E, C, N = 2560, 512, 4, 256, 384
 F32 = mybir.dt.float32
 BF16 = mybir.dt.bfloat16
 U32 = mybir.dt.uint32
+I32 = mybir.dt.int32
 U16 = mybir.dt.uint16
 U8 = mybir.dt.uint8
 FP8X4 = mybir.dt.float8_e4m3fn_x4
@@ -28,7 +29,7 @@ LIST_ROWS = 16
 FLOPS = 2 * K * N * E * C
 
 PLANES_PER_TILE = 4
-SLOT_SLICES = {1: ((0, 384), (384, 768), (768, 1024)), 2: ((0, 768), (768, 1024)), 3: ((0, 1024),)}
+WINDOW = 3 * T
 
 SHARED = 0.4
 
@@ -37,6 +38,7 @@ SCALAR_UNITS = (0, 1, 2, 3, 4, 5, 6, 10, 14)
 HALVED_UNITS = (11, 15, 17)
 BIAS_UNIT = 8
 WHOLE_UNITS = UNITS - 1
+DMA_ALIGN = 256
 RAW_BUFS = 7
 GROUP_BUFS = 3
 GROUPED_BUFS = 10
@@ -69,9 +71,10 @@ def tile_routed_moe_kernel(tc, xT, w, b, gate, offs, pos1, pos2, out):
         pos1_list = keep.tile([P, T // LIST_ROWS], U16, name="pos1_list")
         pos2_list = keep.tile([P, T // LIST_ROWS], U16, name="pos2_list")
 
-        token_codes = keep.tile([P, PASSES * T], U32, name="token_codes", align_bytes=64)
-        token_scales = keep.tile([P, 2 * T], U8, name="token_scales", align_bytes=64)
-        nc.gpsimd.memset(token_scales[:], 0)
+        token_codes = keep.tile([P, (PASSES - 1) * T + WINDOW], U32, name="token_codes", align_bytes=64)
+        nc.vector.memset(token_codes[:, PASSES * T :].bitcast(I32), 0)
+        token_scales = keep.tile([P, T + WINDOW], U8, name="token_scales", align_bytes=64)
+        nc.vector.memset(token_scales[:].bitcast(I32), 0)
         slot_scales = []
         for i in range(0, PASSES, PLANES_PER_TILE):
             slots = keep.tile([P, SLOTS], U8, name=f"slot_scales{i}", align_bytes=64)
@@ -81,9 +84,9 @@ def tile_routed_moe_kernel(tc, xT, w, b, gate, offs, pos1, pos2, out):
 
         def load_units(units):
             if len(units) == 1:
-                raw = ring.tile([P, 1, PACK, N], F32, name="w_single", tag="raw", bufs=RAW_BUFS)
+                raw = ring.tile([P, 1, PACK, N], F32, name="w_single", tag="raw", bufs=RAW_BUFS, align_bytes=DMA_ALIGN)
             else:
-                raw = ring.tile([P, len(units), PACK, N], F32, name="w_group", tag="group", bufs=GROUP_BUFS)
+                raw = ring.tile([P, len(units), PACK, N], F32, name="w_group", tag="group", bufs=GROUP_BUFS, align_bytes=DMA_ALIGN)
             nc.sync.dma_start(out=raw[:], in_=w_units[:, units[0] : units[-1] + 1])
             for i, unit in enumerate(units):
                 w_raw[unit] = raw[:, i]
@@ -92,16 +95,14 @@ def tile_routed_moe_kernel(tc, xT, w, b, gate, offs, pos1, pos2, out):
         for a in range(PASSES):
             if a == PASSES - 1:
                 load_units(LOADS[0])
-            raw = ring.tile([P, PACK, T], F32, name="x_raw", tag="raw", bufs=RAW_BUFS)
+            raw = ring.tile([P, PACK, T], F32, name="x_raw", tag="raw", bufs=RAW_BUFS, align_bytes=DMA_ALIGN)
             nc.sync.dma_start(out=raw[:], in_=x_rows[a])
             x_raw.append(raw)
             if a == 0:
                 nc.sync.dma_start(out=offs_list[:], in_=offs)
 
-        def gather(dst, tokens, start, width):
-            for lo, hi in SLOT_SLICES[width]:
-                offsets = offs_list[:, lo // LIST_ROWS : hi // LIST_ROWS]
-                nc.vector.tensor_copy(out=dst[:, lo:hi], in_=tokens[:, start : start + width * T].indirect(offsets))
+        def gather(dst, tokens, start):
+            nc.vector.tensor_copy(out=dst[:], in_=tokens[:, start : start + WINDOW].indirect(offs_list[:]))
 
         slot_codes = []
         for a in range(PASSES):
@@ -117,10 +118,10 @@ def tile_routed_moe_kernel(tc, xT, w, b, gate, offs, pos1, pos2, out):
                 in_=grouped[:],
             )
             slots = keep.tile([P, SLOTS], U32, name=f"slot_codes{a}", align_bytes=64)
-            gather(slots, token_codes, start, min(a + 1, 3))
+            gather(slots, token_codes, start)
             slot_codes.append(slots)
             if a % PLANES_PER_TILE == PLANES_PER_TILE - 1 or a == PASSES - 1:
-                gather(slot_scales[group], token_scales, scale_start, group + 1)
+                gather(slot_scales[group], token_scales, scale_start)
 
         def multiply(sums, e, a, codes, scales):
             slots = slice(e * C, (e + 1) * C)
@@ -182,8 +183,8 @@ def tile_routed_moe_kernel(tc, xT, w, b, gate, offs, pos1, pos2, out):
             if units[0] > 0:
                 load_units(units)
             if BIAS_UNIT in units:
-                bias = keep.tile([P, BLOCKS, E], F32, name="bias")
-                nc.sync.dma_start(out=bias[:], in_=b.rearrange("(n p) e -> p n e", p=P))
+                bias = keep.tile([P, BLOCKS, 2 * E], F32, name="bias")
+                nc.sync.dma_start(out=bias[:, :, :E], in_=b.rearrange("(n p) e -> p n e", p=P))
             grouped = {}
             for unit in units:
                 tile = ring.tile([P, N * PACK], BF16, name="w_grouped", tag="grouped", bufs=GROUPED_BUFS, align_bytes=64)
@@ -217,17 +218,17 @@ def tile_routed_moe_kernel(tc, xT, w, b, gate, offs, pos1, pos2, out):
         grouped = ring.tile([P, N * PACK], BF16, name="w_grouped", tag="grouped", bufs=GROUPED_BUFS, align_bytes=64)
         codes = ring.tile([P, N], U32, name="w_codes", tag="w_codes", bufs=CODE_BUFS, align_bytes=64)
         scales = ring.tile([P, N], U8, name="w_scales", tag="w_scales", bufs=CODE_BUFS, align_bytes=64)
-        first = ring.tile([P, PACK, P], F32, name="w_first", tag="raw", bufs=RAW_BUFS)
+        first = ring.tile([P, PACK, P], F32, name="w_first", tag="raw", bufs=RAW_BUFS, align_bytes=DMA_ALIGN)
         nc.sync.dma_start(out=first[:], in_=w_rows[e, a, :, :, :P])
-        rest = ring.tile([P, PACK, N - P], F32, name="w_rest", tag="raw", bufs=RAW_BUFS)
+        rest = ring.tile([P, PACK, N - P], F32, name="w_rest", tag="raw", bufs=RAW_BUFS, align_bytes=DMA_ALIGN)
         nc.sync.dma_start(out=rest[:], in_=w_rows[e, a, :, :, P:])
         nc.sync.dma_start(out=pos2_list[:], in_=pos2)
         nc.sync.dma_start(out=pos1_list[:], in_=pos1)
         gates = []
         for n in range(BLOCKS):
-            gate_block = ring.tile([P, 2, T], F32, name="gate_block", tag="raw", bufs=RAW_BUFS)
+            gate_block = ring.tile([P, 2, T], F32, name="gate_block", tag="raw", bufs=RAW_BUFS, align_bytes=DMA_ALIGN)
             rows = gate[:, n * P : (n + 1) * P, :].rearrange("r p t -> p r t")
-            if n == 0:
+            if n < BLOCKS - 1:
                 for r in range(2):
                     nc.sync.dma_start(out=gate_block[:, r, :], in_=rows[:, r, :])
             else:
@@ -236,7 +237,7 @@ def tile_routed_moe_kernel(tc, xT, w, b, gate, offs, pos1, pos2, out):
 
         fetched = []
         for n in range(BLOCKS):
-            both = ring.tile([P, 2, T], F32, name="fetched", tag="fetched", bufs=BLOCKS)
+            both = ring.tile([P, 2, T], F32, name="fetched", tag="fetched", bufs=BLOCKS, align_bytes=DMA_ALIGN)
             fetched.append(both)
         lists = (pos1_list, pos2_list)
 

@@ -16,7 +16,6 @@ SQUARE = mybir.ActivationFunctionType.Square
 COPY = mybir.ActivationFunctionType.Copy
 MULT = mybir.AluOpType.mult
 ADD = mybir.AluOpType.add
-MAX = mybir.AluOpType.max
 
 P = 128
 PACK = 4
@@ -31,29 +30,32 @@ FLOPS = 2 * K * N * E * C
 PLANES_PER_TILE = 4
 WINDOW = 3 * T
 
-SHARED = 0.4
-
-LOADS = ((0,), (1, 2), (3, 4, 5), (6, 7, 8), (9, 10, 11), (12, 13), (14,), (15,), (16,), (17,), (18,))
-SCALAR_UNITS = (0, 1, 2, 3, 4, 5, 6, 10, 14)
-HALVED_UNITS = (11, 15, 17)
+SHARED_TOKENS = 208
+X_LOADS = ((0,), (1,), (2,), (3, 4))
+LOADS = ((0, 1, 2), (3, 4), (5, 6), (7, 8), (9, 10), (11, 12), (13,), (14,), (15,), (16,), (17,))
+GPSIMD_UNITS = (0, 1, 2, 3, 4, 5)
+SCALAR_UNITS = (6, 7, 10, 13)
+HALVED_UNITS = (14,)
+LEAD_UNITS = (15, 17)
+SPLIT_UNIT = 16
 BIAS_UNIT = 8
-WHOLE_UNITS = UNITS - 1
+HELD_UNIT = 14
 DMA_ALIGN = 256
-RAW_BUFS = 7
-GROUP_BUFS = 3
-GROUPED_BUFS = 10
-CODE_BUFS = 10
+RAW_BUFS = 5
+GROUP_BUFS = 4
+GROUPED_BUFS = 9
+CODE_BUFS = 9
 
 
-def interleave(nc, grouped, raw, scalar_share):
+def interleave(nc, engine, grouped, raw):
     dst = grouped.rearrange("p (c i t) -> p c t i", i=4, t=PACK)
     src = raw.rearrange("p t (c i) -> p c t i", i=4)
-    quads = dst.shape[1]
-    cut = 2 * int(quads * scalar_share / 2 + 0.5)
-    if cut > 0:
-        nc.scalar.copy(out=dst[:, :cut], in_=src[:, :cut])
-    if cut < quads:
-        nc.vector.tensor_copy(out=dst[:, cut:], in_=src[:, cut:])
+    if engine == "scalar":
+        nc.scalar.copy(out=dst, in_=src)
+    elif engine == "vector":
+        nc.vector.tensor_copy(out=dst, in_=src)
+    else:
+        nc.gpsimd.tensor_scalar(out=dst, in0=src, scalar1=1.0, scalar2=0.0, op0=MULT, op1=ADD)
 
 
 def tile_routed_moe_kernel(tc, xT, w, b, gate, offs, pos1, pos2, out):
@@ -63,7 +65,7 @@ def tile_routed_moe_kernel(tc, xT, w, b, gate, offs, pos1, pos2, out):
         ring = ctx.enter_context(tc.tile_pool(name="ring", bufs=2))
         psum = ctx.enter_context(tc.psum_pool(name="psum", bufs=8))
 
-        x_rows = xT.rearrange("(a p j) t -> a p j t", p=P, j=PACK)
+        x_rows = xT.rearrange("(a p j) t -> p a j t", p=P, j=PACK)
         w_rows = w.rearrange("e (a p j) n -> e a p j n", p=P, j=PACK)
         w_units = w.rearrange("e (a p j) n -> p (e a) j n", p=P, j=PACK)
 
@@ -79,8 +81,18 @@ def tile_routed_moe_kernel(tc, xT, w, b, gate, offs, pos1, pos2, out):
         for i in range(0, PASSES, PLANES_PER_TILE):
             slots = keep.tile([P, SLOTS], U8, name=f"slot_scales{i}", align_bytes=64)
             slot_scales.append(slots)
+        y = []
+        for n in range(BLOCKS):
+            y_block = keep.tile([P, SLOTS], F32, name=f"y{n}")
+            y.append(y_block)
+        bias = keep.tile([P, BLOCKS, 2 * E], F32, name="bias")
 
         w_raw = {}
+        w_grouped = {}
+        w_codes = {}
+        w_scales = {}
+        sums = {}
+        slot_codes = []
 
         def load_units(units):
             if len(units) == 1:
@@ -91,23 +103,86 @@ def tile_routed_moe_kernel(tc, xT, w, b, gate, offs, pos1, pos2, out):
             for i, unit in enumerate(units):
                 w_raw[unit] = raw[:, i]
 
-        x_raw = []
-        for a in range(PASSES):
-            if a == PASSES - 1:
-                load_units(LOADS[0])
-            raw = ring.tile([P, PACK, T], F32, name="x_raw", tag="raw", bufs=RAW_BUFS, align_bytes=DMA_ALIGN)
-            nc.sync.dma_start(out=raw[:], in_=x_rows[a])
-            x_raw.append(raw)
+        def open_unit(unit):
+            w_grouped[unit] = ring.tile(
+                [P, N * PACK], BF16, name="w_grouped", tag="grouped", bufs=GROUPED_BUFS, align_bytes=64
+            )
+            w_codes[unit] = ring.tile([P, N], U32, name="w_codes", tag="w_codes", bufs=CODE_BUFS, align_bytes=64)
+            w_scales[unit] = ring.tile([P, N], U8, name="w_scales", tag="w_scales", bufs=CODE_BUFS, align_bytes=64)
+
+        def interleave_unit(unit):
+            open_unit(unit)
+            if unit in SCALAR_UNITS:
+                pieces = ((0, N, "scalar"),)
+            elif unit in HALVED_UNITS:
+                pieces = ((0, N // 2, "scalar"), (N // 2, N, "vector"))
+            elif unit in GPSIMD_UNITS:
+                pieces = ((0, P, "gpsimd"), (P, N, "scalar"))
+            elif unit in LEAD_UNITS:
+                pieces = ((0, P, "scalar"), (P, N, "vector"))
+            elif unit == SPLIT_UNIT:
+                pieces = ((0, 2 * P, "vector"), (2 * P, N, "vector"))
+            else:
+                pieces = ((0, N, "vector"),)
+            for lo, hi, engine in pieces:
+                interleave(nc, engine, w_grouped[unit][:, PACK * lo : PACK * hi], w_raw[unit][:, :, lo:hi])
+
+        def quantise(unit, lo, hi):
+            nc.vector.quantize_mx(
+                out=w_codes[unit][:, lo:hi].bitcast(FP8X4),
+                scales=w_scales[unit][:, lo:hi],
+                in_=w_grouped[unit][:, PACK * lo : PACK * hi],
+            )
+
+        def multiply(unit, n):
+            e, a = unit // PASSES, unit % PASSES
             if a == 0:
-                nc.sync.dma_start(out=offs_list[:], in_=offs)
+                bank = psum.tile([P, C], F32, name="bank", tag="bank")
+                sums[(e, n)] = bank[:]
+            slots = slice(e * C, (e + 1) * C)
+            features = slice(n * P, (n + 1) * P)
+            plane = PACK * (a % PLANES_PER_TILE)
+            nc.tensor.matmul_mx(
+                out=sums[(e, n)],
+                lhsT=w_codes[unit][:, features].bitcast(FP8X4),
+                lhsT_scale=w_scales[unit][:, features],
+                rhs=slot_codes[a][:, slots].bitcast(FP8X4),
+                rhs_scale=slot_scales[a // PLANES_PER_TILE][plane:P, slots],
+                start=(a == 0),
+                stop=(a == PASSES - 1),
+            )
+
+        def relu(e, n, lo, hi):
+            part = y[n][:, e * C + lo : e * C + hi]
+            nc.scalar.activation(out=part, in_=sums[(e, n)][:, lo:hi], func=RELU, bias=bias[:, n, e : e + 1])
+
+        def square(e, n, lo, hi):
+            part = y[n][:, e * C + lo : e * C + hi]
+            nc.scalar.activation(out=part, in_=part, func=SQUARE)
 
         def gather(dst, tokens, start):
             nc.vector.tensor_copy(out=dst[:], in_=tokens[:, start : start + WINDOW].indirect(offs_list[:]))
 
-        slot_codes = []
+        x_raw = []
+        for passes in X_LOADS:
+            if len(passes) == 1:
+                raw = ring.tile([P, 1, PACK, T], F32, name="x_single", tag="raw", bufs=RAW_BUFS, align_bytes=DMA_ALIGN)
+            else:
+                raw = ring.tile(
+                    [P, len(passes), PACK, T], F32, name="x_group", tag="group", bufs=GROUP_BUFS, align_bytes=DMA_ALIGN
+                )
+            nc.sync.dma_start(out=raw[:], in_=x_rows[:, passes[0] : passes[-1] + 1])
+            for i in range(len(passes)):
+                x_raw.append(raw[:, i])
+            if passes[0] == 0:
+                nc.sync.dma_start(out=offs_list[:], in_=offs)
+
         for a in range(PASSES):
             grouped = ring.tile([P, T * PACK], BF16, name="x_grouped", tag="grouped", bufs=GROUPED_BUFS, align_bytes=64)
-            interleave(nc, grouped[:], x_raw[a][:], SHARED if a == 0 else 1)
+            cut = SHARED_TOKENS if a == 0 else T
+            interleave(nc, "scalar", grouped[:, : PACK * cut], x_raw[a][:, :, :cut])
+            if cut < T:
+                interleave(nc, "vector", grouped[:, PACK * cut :], x_raw[a][:, :, cut:])
             start = (PASSES - 1 - a) * T
             plane = PACK * (a % PLANES_PER_TILE)
             group = a // PLANES_PER_TILE
@@ -123,106 +198,46 @@ def tile_routed_moe_kernel(tc, xT, w, b, gate, offs, pos1, pos2, out):
             if a % PLANES_PER_TILE == PLANES_PER_TILE - 1 or a == PASSES - 1:
                 gather(slot_scales[group], token_scales, scale_start)
 
-        def multiply(sums, e, a, codes, scales):
-            slots = slice(e * C, (e + 1) * C)
-            plane = PACK * (a % PLANES_PER_TILE)
-            nc.tensor.matmul_mx(
-                out=sums,
-                lhsT=codes.bitcast(FP8X4),
-                lhsT_scale=scales,
-                rhs=slot_codes[a][:, slots].bitcast(FP8X4),
-                rhs_scale=slot_scales[a // PLANES_PER_TILE][plane:P, slots],
-                start=(a == 0),
-                stop=(a == PASSES - 1),
-            )
-
-        y = []
-        for n in range(BLOCKS):
-            y_block = keep.tile([P, SLOTS], F32, name=f"y{n}")
-            y.append(y_block)
-
-        def relu(engine, bias, sums, e, n):
-            part = y[n][:, e * C : (e + 1) * C]
-            if engine == "scalar":
-                nc.scalar.activation(out=part, in_=sums, func=RELU, bias=bias[:, n, e : e + 1])
-            else:
-                nc.vector.tensor_scalar(
-                    out=part, in0=sums, scalar1=bias[:, n, e : e + 1], scalar2=0.0, op0=ADD, op1=MAX
-                )
-
-        def square(engine, first_expert, last_expert, n):
-            part = y[n][:, first_expert * C : (last_expert + 1) * C]
-            if engine == "scalar":
-                nc.scalar.activation(out=part, in_=part, func=SQUARE)
-            else:
-                nc.vector.tensor_tensor(out=part, in0=part, in1=part, op=MULT)
-
-        def pieces_of(unit):
-            if unit in SCALAR_UNITS:
-                return ((0, N, 1),)
-            if unit == WHOLE_UNITS - 1:
-                return ((0, P, 1), (P, N, 0))
-            if unit in HALVED_UNITS:
-                return ((0, N, 0.5),)
-            if unit >= LOADS[7][0]:
-                return ((0, 2 * P, 0), (2 * P, N, 0))
-            return ((0, N, 0),)
-
-        sums = {}
         closed = []
 
         def empty_banks():
-            for e in closed:
-                for n in range(BLOCKS):
-                    relu("scalar", bias, sums[(e, n)], e, n)
-            for n in range(BLOCKS):
-                square("scalar", closed[0], closed[-1], n)
+            for expert in closed:
+                for step in (relu, square):
+                    for n in range(BLOCKS):
+                        step(expert, n, 0, C)
             closed.clear()
 
         for units in LOADS:
-            if units[0] > 0:
-                load_units(units)
+            load_units(units)
             if BIAS_UNIT in units:
-                bias = keep.tile([P, BLOCKS, 2 * E], F32, name="bias")
                 nc.sync.dma_start(out=bias[:, :, :E], in_=b.rearrange("(n p) e -> p n e", p=P))
-            grouped = {}
             for unit in units:
-                tile = ring.tile([P, N * PACK], BF16, name="w_grouped", tag="grouped", bufs=GROUPED_BUFS, align_bytes=64)
-                grouped[unit] = tile
-                for lo, hi, share in pieces_of(unit):
-                    interleave(nc, tile[:, PACK * lo : PACK * hi], w_raw[unit][:, :, lo:hi], share)
-            if units[0] == LOADS[7][0]:
+                interleave_unit(unit)
+            if units[0] == HELD_UNIT + 1:
                 empty_banks()
             for unit in units:
-                e, a = unit // PASSES, unit % PASSES
-                codes = ring.tile([P, N], U32, name="w_codes", tag="w_codes", bufs=CODE_BUFS, align_bytes=64)
-                scales = ring.tile([P, N], U8, name="w_scales", tag="w_scales", bufs=CODE_BUFS, align_bytes=64)
-                for lo, hi, share in pieces_of(unit):
-                    nc.vector.quantize_mx(
-                        out=codes[:, lo:hi].bitcast(FP8X4),
-                        scales=scales[:, lo:hi],
-                        in_=grouped[unit][:, PACK * lo : PACK * hi],
-                    )
+                cut = 2 * P if unit == SPLIT_UNIT else P if unit in LEAD_UNITS else 0
+                for lo, hi in ((0, cut), (cut, N)) if cut else ((0, N),):
+                    quantise(unit, lo, hi)
                 for n in range(BLOCKS):
-                    if a == 0:
-                        bank = psum.tile([P, C], F32, name="bank", tag="bank")
-                        sums[(e, n)] = bank[:]
-                    features = slice(n * P, (n + 1) * P)
-                    multiply(sums[(e, n)], e, a, codes[:, features], scales[:, features])
-                if a == PASSES - 1:
-                    closed.append(e)
-            if closed and closed[0] < E - 2 and units[-1] >= BIAS_UNIT:
+                    multiply(unit, n)
+                if unit % PASSES == PASSES - 1:
+                    closed.append(unit // PASSES)
+            if BIAS_UNIT <= units[-1] < HELD_UNIT:
                 empty_banks()
 
-        e, a = E - 1, PASSES - 1
-        grouped = ring.tile([P, N * PACK], BF16, name="w_grouped", tag="grouped", bufs=GROUPED_BUFS, align_bytes=64)
-        codes = ring.tile([P, N], U32, name="w_codes", tag="w_codes", bufs=CODE_BUFS, align_bytes=64)
-        scales = ring.tile([P, N], U8, name="w_scales", tag="w_scales", bufs=CODE_BUFS, align_bytes=64)
-        first = ring.tile([P, PACK, P], F32, name="w_first", tag="raw", bufs=RAW_BUFS, align_bytes=DMA_ALIGN)
-        nc.sync.dma_start(out=first[:], in_=w_rows[e, a, :, :, :P])
-        rest = ring.tile([P, PACK, N - P], F32, name="w_rest", tag="raw", bufs=RAW_BUFS, align_bytes=DMA_ALIGN)
-        nc.sync.dma_start(out=rest[:], in_=w_rows[e, a, :, :, P:])
-        nc.sync.dma_start(out=pos2_list[:], in_=pos2)
+        e = E - 1
+        late = (UNITS - 2, UNITS - 1)
+        leads = {}
+        for unit in late:
+            leads[unit] = ring.tile([P, PACK, P], F32, name="w_lead", tag="lead", bufs=2, align_bytes=DMA_ALIGN)
+            nc.sync.dma_start(out=leads[unit][:], in_=w_rows[e, unit % PASSES, :, :, :P])
+        trails = {}
+        for unit in late:
+            trails[unit] = ring.tile([P, PACK, N - P], F32, name="w_trail", tag="raw", bufs=RAW_BUFS, align_bytes=DMA_ALIGN)
+            nc.sync.dma_start(out=trails[unit][:], in_=w_rows[e, unit % PASSES, :, :, P:])
+            if unit == late[0]:
+                nc.sync.dma_start(out=pos2_list[:], in_=pos2)
         nc.sync.dma_start(out=pos1_list[:], in_=pos1)
         gates = []
         for n in range(BLOCKS):
@@ -240,15 +255,6 @@ def tile_routed_moe_kernel(tc, xT, w, b, gate, offs, pos1, pos2, out):
             both = ring.tile([P, 2, T], F32, name="fetched", tag="fetched", bufs=BLOCKS, align_bytes=DMA_ALIGN)
             fetched.append(both)
         lists = (pos1_list, pos2_list)
-
-        def close_block(n):
-            features = slice(n * P, (n + 1) * P)
-            nc.vector.quantize_mx(
-                out=codes[:, features].bitcast(FP8X4),
-                scales=scales[:, features],
-                in_=grouped[:, PACK * n * P : PACK * (n + 1) * P],
-            )
-            multiply(sums[(e, n)], e, a, codes[:, features], scales[:, features])
 
         def fetch(n, r, lo, hi):
             offsets = lists[r][:, lo // LIST_ROWS : hi // LIST_ROWS]
@@ -268,24 +274,25 @@ def tile_routed_moe_kernel(tc, xT, w, b, gate, offs, pos1, pos2, out):
             nc.vector.tensor_tensor(out=part, in0=part, in1=fetched[n][:, 1, lo:hi], op=ADD)
             nc.sync.dma_start(out=out[n * P : (n + 1) * P, lo:hi], in_=part)
 
-        interleave(nc, grouped[:, : PACK * P], first[:], 1)
-        close_block(0)
-        for func in (RELU, SQUARE):
+        for unit in late:
+            open_unit(unit)
+            interleave(nc, "scalar", w_grouped[unit][:, : PACK * P], leads[unit][:])
+            quantise(unit, 0, P)
+            multiply(unit, 0)
+        for step in (relu, square):
             for lo, hi in ((0, C // 2), (C // 2, C)):
-                part = y[0][:, e * C + lo : e * C + hi]
-                if func == RELU:
-                    nc.scalar.activation(out=part, in_=sums[(e, 0)][:, lo:hi], func=RELU, bias=bias[:, 0, e : e + 1])
-                else:
-                    nc.scalar.activation(out=part, in_=part, func=SQUARE)
+                step(e, 0, lo, hi)
         fetch(0, 1, 0, T)
-        for n in (1, 2):
-            interleave(nc, grouped[:, PACK * n * P : PACK * (n + 1) * P], rest[:, :, (n - 1) * P : n * P], 0)
-        for n in (1, 2):
-            close_block(n)
-        for n in (1, 2):
-            relu("scalar", bias, sums[(e, n)], e, n)
-        for n in (1, 2):
-            square("scalar", e, e, n)
+        for unit in late:
+            for n in (1, 2):
+                part = trails[unit][:, :, (n - 1) * P : n * P]
+                interleave(nc, "vector", w_grouped[unit][:, PACK * n * P : PACK * (n + 1) * P], part)
+            for n in (1, 2):
+                quantise(unit, n * P, (n + 1) * P)
+                multiply(unit, n)
+        for step in (relu, square):
+            for n in (1, 2):
+                step(e, n, 0, C)
 
         halves = ((0, T // 2), (T // 2, T))
         fetch_weighted(0)

@@ -36,7 +36,8 @@ LOADS = ((0, 1, 2), (3, 4), (5, 6), (7, 8), (9, 10), (11, 12), (13,), (14,), (15
 GPSIMD_UNITS = (0, 1, 2, 3, 4, 5)
 SCALAR_UNITS = (6, 7, 10, 13)
 HALVED_UNITS = (14,)
-LEAD_UNITS = (15, 17)
+TAIL_UNITS = (15,)
+LEAD_UNITS = (17,)
 SPLIT_UNIT = 16
 BIAS_UNIT = 8
 HELD_UNIT = 14
@@ -116,6 +117,8 @@ def tile_routed_moe_kernel(tc, xT, w, b, gate, offs, pos1, pos2, out):
                 pieces = ((0, N, "scalar"),)
             elif unit in HALVED_UNITS:
                 pieces = ((0, N // 2, "scalar"), (N // 2, N, "vector"))
+            elif unit in TAIL_UNITS:
+                pieces = ((0, 2 * P, "scalar"), (2 * P, N, "vector"))
             elif unit in GPSIMD_UNITS:
                 pieces = ((0, P, "gpsimd"), (P, N, "scalar"))
             elif unit in LEAD_UNITS:
@@ -279,6 +282,7 @@ def tile_routed_moe_kernel(tc, xT, w, b, gate, offs, pos1, pos2, out):
             interleave(nc, "scalar", w_grouped[unit][:, : PACK * P], leads[unit][:])
             quantise(unit, 0, P)
             multiply(unit, 0)
+        interleave(nc, "scalar", w_grouped[late[0]][:, PACK * P : PACK * 2 * P], trails[late[0]][:, :, :P])
         for step in (relu, square):
             for lo, hi in ((0, C // 2), (C // 2, C)):
                 step(e, 0, lo, hi)
@@ -286,8 +290,9 @@ def tile_routed_moe_kernel(tc, xT, w, b, gate, offs, pos1, pos2, out):
         for unit in late:
             for n in (1, 2):
                 part = trails[unit][:, :, (n - 1) * P : n * P]
-                interleave(nc, "vector", w_grouped[unit][:, PACK * n * P : PACK * (n + 1) * P], part)
-            for n in (1, 2):
+                if (unit, n) != (late[0], 1):
+                    interleave(nc, "vector", w_grouped[unit][:, PACK * n * P : PACK * (n + 1) * P], part)
+            for n in (2, 1) if unit == late[0] else (1, 2):
                 quantise(unit, n * P, (n + 1) * P)
                 multiply(unit, n)
         for step in (relu, square):

from contextlib import ExitStack

import concourse.mybir as mybir

K, T, E, C, N = 2560, 512, 4, 256, 384

F32 = mybir.dt.float32
BF16 = mybir.dt.bfloat16
U32 = mybir.dt.uint32
I32 = mybir.dt.int32
U16 = mybir.dt.uint16
U8 = mybir.dt.uint8
FP8X4 = mybir.dt.float8_e4m3fn_x4
RELU = mybir.ActivationFunctionType.Relu
SQUARE = mybir.ActivationFunctionType.Square
COPY = mybir.ActivationFunctionType.Copy
MULT = mybir.AluOpType.mult
ADD = mybir.AluOpType.add

P = 128
PACK = 4
PASSES = K // (P * PACK)
BLOCKS = N // P
SLOTS = E * C
UNITS = E * PASSES
LIST_ROWS = 16

FLOPS = 2 * K * N * E * C

PLANES_PER_TILE = 4
WINDOW = 3 * T

SHARED_TOKENS = 208
X_LOADS = ((0,), (1,), (2,), (3, 4))
LOADS = ((0, 1, 2), (3, 4), (5, 6), (7, 8), (9, 10), (11, 12), (13,), (14,), (15,), (16,), (17,))
GPSIMD_UNITS = (0, 1, 2, 3, 4, 5)
SCALAR_UNITS = (6, 7, 10, 13)
HALVED_UNITS = (14,)
TAIL_UNITS = (15,)
LEAD_UNITS = (17,)
SPLIT_UNIT = 16
BIAS_UNIT = 8
HELD_UNIT = 14
DMA_ALIGN = 256
RAW_BUFS = 5
GROUP_BUFS = 4
GROUPED_BUFS = 9
CODE_BUFS = 9


def interleave(nc, engine, grouped, raw):
    dst = grouped.rearrange("p (c i t) -> p c t i", i=4, t=PACK)
    src = raw.rearrange("p t (c i) -> p c t i", i=4)
    if engine == "scalar":
        nc.scalar.copy(out=dst, in_=src)
    elif engine == "vector":
        nc.vector.tensor_copy(out=dst, in_=src)
    else:
        nc.gpsimd.tensor_scalar(out=dst, in0=src, scalar1=1.0, scalar2=0.0, op0=MULT, op1=ADD)


def tile_routed_moe_kernel(tc, xT, w, b, gate, offs, pos1, pos2, out):
    nc = tc.nc
    with ExitStack() as ctx:
        keep = ctx.enter_context(tc.tile_pool(name="keep", bufs=1))
        ring = ctx.enter_context(tc.tile_pool(name="ring", bufs=2))
        psum = ctx.enter_context(tc.psum_pool(name="psum", bufs=8))

        x_rows = xT.rearrange("(a p j) t -> p a j t", p=P, j=PACK)
        w_rows = w.rearrange("e (a p j) n -> e a p j n", p=P, j=PACK)
        w_units = w.rearrange("e (a p j) n -> p (e a) j n", p=P, j=PACK)

        offs_list = keep.tile([P, SLOTS // LIST_ROWS], U16, name="offs_list")
        pos1_list = keep.tile([P, T // LIST_ROWS], U16, name="pos1_list")
        pos2_list = keep.tile([P, T // LIST_ROWS], U16, name="pos2_list")

        token_codes = keep.tile([P, (PASSES - 1) * T + WINDOW], U32, name="token_codes", align_bytes=64)
        nc.vector.memset(token_codes[:, PASSES * T :].bitcast(I32), 0)
        token_scales = keep.tile([P, T + WINDOW], U8, name="token_scales", align_bytes=64)
        nc.vector.memset(token_scales[:].bitcast(I32), 0)
        slot_scales = []
        for i in range(0, PASSES, PLANES_PER_TILE):
            slots = keep.tile([P, SLOTS], U8, name=f"slot_scales{i}", align_bytes=64)
            slot_scales.append(slots)
        y = []
        for n in range(BLOCKS):
            y_block = keep.tile([P, SLOTS], F32, name=f"y{n}")
            y.append(y_block)
        bias = keep.tile([P, BLOCKS, 2 * E], F32, name="bias")

        w_raw = {}
        w_grouped = {}
        w_codes = {}
        w_scales = {}
        sums = {}
        slot_codes = []

        def load_units(units):
            if len(units) == 1:
                raw = ring.tile([P, 1, PACK, N], F32, name="w_single", tag="raw", bufs=RAW_BUFS, align_bytes=DMA_ALIGN)
            else:
                raw = ring.tile([P, len(units), PACK, N], F32, name="w_group", tag="group", bufs=GROUP_BUFS, align_bytes=DMA_ALIGN)
            nc.sync.dma_start(out=raw[:], in_=w_units[:, units[0] : units[-1] + 1])
            for i, unit in enumerate(units):
                w_raw[unit] = raw[:, i]

        def open_unit(unit):
            w_grouped[unit] = ring.tile(
                [P, N * PACK], BF16, name="w_grouped", tag="grouped", bufs=GROUPED_BUFS, align_bytes=64
            )
            w_codes[unit] = ring.tile([P, N], U32, name="w_codes", tag="w_codes", bufs=CODE_BUFS, align_bytes=64)
            w_scales[unit] = ring.tile([P, N], U8, name="w_scales", tag="w_scales", bufs=CODE_BUFS, align_bytes=64)

        def interleave_unit(unit):
            open_unit(unit)
            if unit in SCALAR_UNITS:
                pieces = ((0, N, "scalar"),)
            elif unit in HALVED_UNITS:
                pieces = ((0, N // 2, "scalar"), (N // 2, N, "vector"))
            elif unit in TAIL_UNITS:
                pieces = ((0, 2 * P, "scalar"), (2 * P, N, "vector"))
            elif unit in GPSIMD_UNITS:
                pieces = ((0, P, "gpsimd"), (P, N, "scalar"))
            elif unit in LEAD_UNITS:
                pieces = ((0, P, "scalar"), (P, N, "vector"))
            elif unit == SPLIT_UNIT:
                pieces = ((0, 2 * P, "vector"), (2 * P, N, "vector"))
            else:
                pieces = ((0, N, "vector"),)
            for lo, hi, engine in pieces:
                interleave(nc, engine, w_grouped[unit][:, PACK * lo : PACK * hi], w_raw[unit][:, :, lo:hi])

        def quantise(unit, lo, hi):
            nc.vector.quantize_mx(
                out=w_codes[unit][:, lo:hi].bitcast(FP8X4),
                scales=w_scales[unit][:, lo:hi],
                in_=w_grouped[unit][:, PACK * lo : PACK * hi],
            )

        def multiply(unit, n):
            e, a = unit // PASSES, unit % PASSES
            if a == 0:
                bank = psum.tile([P, C], F32, name="bank", tag="bank")
                sums[(e, n)] = bank[:]
            slots = slice(e * C, (e + 1) * C)
            features = slice(n * P, (n + 1) * P)
            plane = PACK * (a % PLANES_PER_TILE)
            nc.tensor.matmul_mx(
                out=sums[(e, n)],
                lhsT=w_codes[unit][:, features].bitcast(FP8X4),
                lhsT_scale=w_scales[unit][:, features],
                rhs=slot_codes[a][:, slots].bitcast(FP8X4),
                rhs_scale=slot_scales[a // PLANES_PER_TILE][plane:P, slots],
                start=(a == 0),
                stop=(a == PASSES - 1),
            )

        def relu(e, n, lo, hi):
            part = y[n][:, e * C + lo : e * C + hi]
            nc.scalar.activation(out=part, in_=sums[(e, n)][:, lo:hi], func=RELU, bias=bias[:, n, e : e + 1])

        def square(e, n, lo, hi):
            part = y[n][:, e * C + lo : e * C + hi]
            nc.scalar.activation(out=part, in_=part, func=SQUARE)

        def gather(dst, tokens, start):
            nc.vector.tensor_copy(out=dst[:], in_=tokens[:, start : start + WINDOW].indirect(offs_list[:]))

        x_raw = []
        for passes in X_LOADS:
            if len(passes) == 1:
                raw = ring.tile([P, 1, PACK, T], F32, name="x_single", tag="raw", bufs=RAW_BUFS, align_bytes=DMA_ALIGN)
            else:
                raw = ring.tile(
                    [P, len(passes), PACK, T], F32, name="x_group", tag="group", bufs=GROUP_BUFS, align_bytes=DMA_ALIGN
                )
            nc.sync.dma_start(out=raw[:], in_=x_rows[:, passes[0] : passes[-1] + 1])
            for i in range(len(passes)):
                x_raw.append(raw[:, i])
            if passes[0] == 0:
                nc.sync.dma_start(out=offs_list[:], in_=offs)

        for a in range(PASSES):
            grouped = ring.tile([P, T * PACK], BF16, name="x_grouped", tag="grouped", bufs=GROUPED_BUFS, align_bytes=64)
            cut = SHARED_TOKENS if a == 0 else T
            interleave(nc, "scalar", grouped[:, : PACK * cut], x_raw[a][:, :, :cut])
            if cut < T:
                interleave(nc, "vector", grouped[:, PACK * cut :], x_raw[a][:, :, cut:])
            start = (PASSES - 1 - a) * T
            plane = PACK * (a % PLANES_PER_TILE)
            group = a // PLANES_PER_TILE
            scale_start = (1 - group) * T
            nc.vector.quantize_mx(
                out=token_codes[:, start : start + T].bitcast(FP8X4),
                scales=token_scales[plane:P, scale_start : scale_start + T],
                in_=grouped[:],
            )
            slots = keep.tile([P, SLOTS], U32, name=f"slot_codes{a}", align_bytes=64)
            gather(slots, token_codes, start)
            slot_codes.append(slots)
            if a % PLANES_PER_TILE == PLANES_PER_TILE - 1 or a == PASSES - 1:
                gather(slot_scales[group], token_scales, scale_start)

        closed = []

        def empty_banks():
            for expert in closed:
                for step in (relu, square):
                    for n in range(BLOCKS):
                        step(expert, n, 0, C)
            closed.clear()

        for units in LOADS:
            load_units(units)
            if BIAS_UNIT in units:
                nc.sync.dma_start(out=bias[:, :, :E], in_=b.rearrange("(n p) e -> p n e", p=P))
            for unit in units:
                interleave_unit(unit)
            if units[0] == HELD_UNIT + 1:
                empty_banks()
            for unit in units:
                cut = 2 * P if unit == SPLIT_UNIT else P if unit in LEAD_UNITS else 0
                for lo, hi in ((0, cut), (cut, N)) if cut else ((0, N),):
                    quantise(unit, lo, hi)
                for n in range(BLOCKS):
                    multiply(unit, n)
                if unit % PASSES == PASSES - 1:
                    closed.append(unit // PASSES)
            if BIAS_UNIT <= units[-1] < HELD_UNIT:
                empty_banks()

        e = E - 1
        late = (UNITS - 2, UNITS - 1)
        leads = {}
        for unit in late:
            leads[unit] = ring.tile([P, PACK, P], F32, name="w_lead", tag="lead", bufs=2, align_bytes=DMA_ALIGN)
            nc.sync.dma_start(out=leads[unit][:], in_=w_rows[e, unit % PASSES, :, :, :P])
        trails = {}
        for unit in late:
            trails[unit] = ring.tile([P, PACK, N - P], F32, name="w_trail", tag="raw", bufs=RAW_BUFS, align_bytes=DMA_ALIGN)
            nc.sync.dma_start(out=trails[unit][:], in_=w_rows[e, unit % PASSES, :, :, P:])
            if unit == late[0]:
                nc.sync.dma_start(out=pos2_list[:], in_=pos2)
        nc.sync.dma_start(out=pos1_list[:], in_=pos1)
        gates = []
        for n in range(BLOCKS):
            gate_block = ring.tile([P, 2, T], F32, name="gate_block", tag="raw", bufs=RAW_BUFS, align_bytes=DMA_ALIGN)
            rows = gate[:, n * P : (n + 1) * P, :].rearrange("r p t -> p r t")
            if n < BLOCKS - 1:
                for r in range(2):
                    nc.sync.dma_start(out=gate_block[:, r, :], in_=rows[:, r, :])
            else:
                nc.sync.dma_start(out=gate_block[:], in_=rows)
            gates.append(gate_block)

        fetched = []
        for n in range(BLOCKS):
            both = ring.tile([P, 2, T], F32, name="fetched", tag="fetched", bufs=BLOCKS, align_bytes=DMA_ALIGN)
            fetched.append(both)
        lists = (pos1_list, pos2_list)

        def fetch(n, r, lo, hi):
            offsets = lists[r][:, lo // LIST_ROWS : hi // LIST_ROWS]
            nc.scalar.activation(out=fetched[n][:, r, lo:hi], in_=y[n][:].indirect(offsets), func=COPY)

        def fetch_weighted(n):
            nc.vector.tensor_tensor(
                out=fetched[n][:, 0, :], in0=y[n][:].indirect(pos1_list[:]), in1=gates[n][:, 0, :], op=MULT
            )

        def weight(n, r, lo, hi):
            part = fetched[n][:, r, lo:hi]
            nc.vector.tensor_tensor(out=part, in0=part, in1=gates[n][:, r, lo:hi], op=MULT)

        def add_and_store(n, lo, hi):
            part = fetched[n][:, 0, lo:hi]
            nc.vector.tensor_tensor(out=part, in0=part, in1=fetched[n][:, 1, lo:hi], op=ADD)
            nc.sync.dma_start(out=out[n * P : (n + 1) * P, lo:hi], in_=part)

        for unit in late:
            open_unit(unit)
            interleave(nc, "scalar", w_grouped[unit][:, : PACK * P], leads[unit][:])
            quantise(unit, 0, P)
            multiply(unit, 0)
        interleave(nc, "scalar", w_grouped[late[0]][:, PACK * P : PACK * 2 * P], trails[late[0]][:, :, :P])
        for step in (relu, square):
            for lo, hi in ((0, C // 2), (C // 2, C)):
                step(e, 0, lo, hi)
        fetch(0, 1, 0, T)
        for unit in late:
            for n in (1, 2):
                part = trails[unit][:, :, (n - 1) * P : n * P]
                if (unit, n) != (late[0], 1):
                    interleave(nc, "vector", w_grouped[unit][:, PACK * n * P : PACK * (n + 1) * P], part)
            for n in (2, 1) if unit == late[0] else (1, 2):
                quantise(unit, n * P, (n + 1) * P)
                multiply(unit, n)
        for step in (relu, square):
            for n in (1, 2):
                step(e, n, 0, C)

        halves = ((0, T // 2), (T // 2, T))
        fetch_weighted(0)
        weight(0, 1, 0, T)
        fetch(1, 1, 0, T)
        fetch_weighted(1)
        add_and_store(0, 0, T)
        weight(1, 1, 0, T)
        fetch(2, 0, 0, T)
        weight(2, 0, 0, T)
        add_and_store(1, 0, T)
        for lo, hi in halves:
            fetch(2, 1, lo, hi)
        for lo, hi in halves:
            weight(2, 1, lo, hi)
        for lo, hi in halves:
            add_and_store(2, lo, hi)
